import numpy as np
import ml_dtypes


def mxq(x, axis, fmt="e4m3"):
    dtype, down = {"e4m3": (ml_dtypes.float8_e4m3fn, 7), "e5m2": (ml_dtypes.float8_e5m2, 14)}[fmt]
    v = np.moveaxis(np.asarray(x, np.float32).astype(ml_dtypes.bfloat16).astype(np.float64), axis, -1)
    blocks = v.reshape(v.shape[:-1] + (-1, 32))
    amax = np.abs(blocks).max(-1, keepdims=True)
    byte = np.maximum(np.where(amax > 0, np.frexp(amax)[1] - 1 + 127, 0) - down, 1)
    scale = np.exp2(byte - 127.0)
    codes = (blocks / scale).astype(np.float32).astype(dtype).astype(np.float64)
    return np.moveaxis((codes * scale).reshape(v.shape), -1, axis)


WIDE = False


def mx_kscale(k, group=512):
    if not WIDE:
        return np.ones(k)
    levels = np.array([10, -10, 5, -5, 0])
    if group != 512:
        return np.exp2(np.random.permutation(np.resize(levels, k // group))).repeat(group)
    if k % 512:
        return np.exp2(np.random.permutation(np.resize(levels, k // 32))).repeat(32)
    a = np.empty((k // 512, 16))
    for p in range(k // 512):
        a[p, :8] = np.random.permutation(np.resize(levels, 8))
        for g in range(8):
            far = levels[np.abs(levels - a[p, g]) >= 10]
            a[p, g + 8] = far[np.random.randint(len(far))]
    return np.exp2(a.ravel()).repeat(32)


def f64(x):
    return np.asarray(x).astype(np.float64)


def striped(idx):
    return np.tile(np.asarray(idx).reshape(-1, 16).T, (8, 1)).astype(np.uint16)


def unstriped(offs):
    return offs[:16].T.reshape(-1).astype(np.int64)


H, KV, D, NQ, N = 2, 2, 256, 512, 512
CAP = 2.0


def setup_inputs():
    n = np.random.standard_normal
    s = mx_kscale(D, 0)[:, None]
    u = mx_kscale(N)
    t = np.random.uniform(0.5, 2.0, N) * u
    v = n((KV, N, 128))
    v[:, :, 127] = 1.0
    return {
        "qT": (n((H, D, NQ)) * s * (0.70 / np.sqrt(D))).astype(np.float32),
        "kT": (n((KV, D, N)) / s).astype(np.float32),
        "t": t.reshape(N, 1).astype(np.float32),
        "v": (v / t[:, None]).astype(np.float32),
        "kb": (0.5 * n((N, 1))).astype(np.float32),
    }


def reference(qT, kT, t, v, kb):
    a = mxq(f64(kT), 1, "e4m3").transpose(0, 2, 1) @ mxq(f64(qT), 1, "e4m3")
    a = a + f64(kb)
    a = CAP * np.tanh(a / CAP)
    p = np.exp(a)
    w = p * f64(t)
    y = mxq(w, 1, "e4m3").transpose(0, 2, 1) @ mxq(f64(v), 1, "e4m3")
    y = y / (y[:, :, 127:128])
    return y

@@ -1,0 +1,258 @@
+from contextlib import ExitStack
+
+import concourse.mybir as mybir
+
+H, D, NQ, N, E = 2, 256, 512, 512, 128
+CAP = 2.0
+FLOPS = 2 * H * N * NQ * D + 2 * H * NQ * N * E
+
+F32 = mybir.dt.float32
+BF16 = mybir.dt.bfloat16
+U32 = mybir.dt.uint32
+U8 = mybir.dt.uint8
+FP8X4 = mybir.dt.float8_e4m3fn_x4
+ACT = mybir.ActivationFunctionType
+ALU = mybir.AluOpType
+
+P = 128
+PACK = 4
+ROWS = D // PACK
+QC = 128
+CHUNKS = NQ // QC
+KP = 4
+KW = N // KP
+RUN = 4
+
+
+def tile_rows_kb_cap_kernel(tc, qT, kT, t, v, kb, out):
+    nc = tc.nc
+    with ExitStack() as ctx:
+        sb = ctx.enter_context(tc.tile_pool(name="sb", bufs=1))
+        ps = ctx.enter_context(tc.psum_pool(name="ps", bufs=1))
+        ctx.enter_context(tc.manual_schedule())
+
+        def tile(name, shape, dtype):
+            return sb.tile(shape, dtype, name=name, align_bytes=64)
+
+        q_rows = qT.rearrange("h (p j) n -> (h p) j n", j=PACK)
+        k_rows = kT.rearrange("h (p j) n -> (h p) j n", j=PACK)
+
+        kb_raw = tile("kb_raw", [P, PACK], F32)
+        t_sb = tile("t_sb", [P, PACK], F32)
+        kb_half = tile("kb_half", [P, PACK], F32)
+        q_raw = [tile("q_raw%d" % c, [P, PACK, QC], F32) for c in range(CHUNKS)]
+        k_raw = [tile("k_raw%d" % c, [P, PACK, KW], F32) for c in range(KP)]
+        v_raw = tile("v_raw", [P, H, PACK, E], F32)
+
+        nc.scalar.dma_start(out=kb_raw[:], in_=kb.rearrange("(p r) o -> p (r o)", r=PACK))
+        nc.scalar.dma_start(out=t_sb[:], in_=t.rearrange("(p r) o -> p (r o)", r=PACK))
+        nc.sync.dma_start(out=q_raw[0][:], in_=q_rows[:, :, 0:QC])
+        for c in range(KP):
+            nc.sync.dma_start(out=k_raw[c][:], in_=k_rows[:, :, c * KW : (c + 1) * KW])
+        nc.sync.dma_start(out=q_raw[1][:], in_=q_rows[:, :, QC : 2 * QC])
+        nc.sync.dma_start(out=v_raw[:], in_=v.rearrange("h (p r) e -> p h r e", r=PACK))
+        for c in range(2, CHUNKS):
+            nc.sync.dma_start(out=q_raw[c][:], in_=q_rows[:, :, c * QC : (c + 1) * QC])
+
+        nc.scalar.mul(kb_half[:], kb_raw[:], 1.0 / CAP)
+
+        def side_by_side(words):
+            return words.rearrange("p (c i) j -> p c j i", i=RUN)
+
+        def by_rows(rows):
+            return rows.rearrange("p j (c i) -> p c j i", i=RUN)
+
+        def quantise(codes, scales, words):
+            nc.vector.quantize_mx(out=codes.bitcast(FP8X4), scales=scales, in_=words.rearrange("p c j -> p (c j)"))
+
+        q_bf = [tile("q_bf%d" % c, [P, QC, PACK], BF16) for c in range(CHUNKS)]
+        q_codes = [tile("q_codes%d" % c, [P, QC], U32) for c in range(CHUNKS)]
+        q_scales = [tile("q_scales%d" % c, [P, QC], U8) for c in range(CHUNKS)]
+        k_bf = tile("k_bf", [P, PACK, P, PACK], BF16)
+        k_codes = [tile("k_codes%d" % r, [P, P], U32) for r in range(PACK)]
+        k_scales = [tile("k_scales%d" % r, [P, P], U8) for r in range(PACK)]
+        v_bf = tile("v_bf", [P, H * E, PACK], BF16)
+        v_codes = tile("v_codes", [P, H * E], U32)
+        v_scales = tile("v_scales", [P, H * E], U8)
+
+        def pack_q(c):
+            nc.vector.tensor_copy(out=side_by_side(q_bf[c][:]), in_=by_rows(q_raw[c][:]))
+
+        def quant_q(c):
+            quantise(q_codes[c][:], q_scales[c][:], q_bf[c][:])
+
+        def pack_k(c):
+            places = KW // PACK
+            nc.vector.tensor_copy(
+                out=k_bf[:, :, c * places : (c + 1) * places, :].rearrange("p r s j -> p s j r"),
+                in_=k_raw[c][:].rearrange("p j (s r) -> p s j r", r=PACK),
+            )
+
+        def quant_k(r):
+            quantise(k_codes[r][:], k_scales[r][:], k_bf[:, r, :, :])
+
+        def pack_v(h):
+            nc.vector.tensor_copy(out=side_by_side(v_bf[:, h * E : (h + 1) * E, :]), in_=by_rows(v_raw[:, h, :, :]))
+
+        def quant_v():
+            quantise(v_codes[:], v_scales[:], v_bf[:])
+
+        units = [(h, c) for c in range(CHUNKS) for h in range(H)]
+        last = len(units) - 1
+        score_banks = [[ps.tile([P, PACK, QC], F32, name="score%d_%d" % (h, b)) for b in range(3)] for h in range(H)]
+        y_banks = [ps.tile([P, CHUNKS, E], F32, name="y%d" % h) for h in range(H)]
+
+        def score_place(u, r):
+            h, c = units[u]
+            bank = min(r, 2) if c == 0 else c - 1
+            return score_banks[h][bank][:, r, :]
+
+        def scores(u, r):
+            h, c = units[u]
+            rows = slice(h * ROWS, (h + 1) * ROWS)
+            nc.tensor.matmul_mx(
+                out=score_place(u, r),
+                lhsT=k_codes[r][rows, :].bitcast(FP8X4),
+                lhsT_scale=k_scales[r][rows, :],
+                rhs=q_codes[c][rows, :].bitcast(FP8X4),
+                rhs_scale=q_scales[c][rows, :],
+                start=True,
+                stop=True,
+            )
+
+        def pieces(u):
+            return [(0, QC // 2), (QC // 2, QC)] if u == last else [(0, QC)]
+
+        capped = {}
+        prob = {}
+        for u in range(len(units)):
+            for a, b in pieces(u):
+                capped[u, a] = tile("capped%d_%d" % (u, a), [P, PACK, b - a], F32)
+                prob[u, a] = tile("prob%d_%d" % (u, a), [P, PACK, b - a], F32)
+        w_bf = [tile("w_bf%d" % u, [P, QC, PACK], BF16) for u in range(len(units))]
+        w_codes = [tile("w_codes%d" % u, [P, QC], U32) for u in range(len(units))]
+        w_scales = [tile("w_scales%d" % u, [P, QC], U8) for u in range(len(units))]
+        inverse = [tile("inverse%d" % u, [P, 1], F32) for u in range(len(units))]
+        result = [tile("result%d" % u, [P, E], F32) for u in range(len(units))]
+
+        def cap(u, r, piece=0):
+            a, b = pieces(u)[piece]
+            nc.scalar.activation(
+                out=capped[u, a][:, r, :], in_=score_place(u, r)[:, a:b], func=ACT.Tanh,
+                bias=kb_half[:, r : r + 1], scale=1.0 / CAP,
+            )
+
+        def cap_all(u, piece=0):
+            for r in range(PACK):
+                cap(u, r, piece)
+
+        def exponentiate(u, piece=0):
+            a, b = pieces(u)[piece]
+            nc.scalar.activation(out=prob[u, a][:], in_=capped[u, a][:], func=ACT.Exp, scale=CAP)
+
+        def weigh(u, piece=0):
+            a, b = pieces(u)[piece]
+            nc.vector.tensor_tensor(
+                out=side_by_side(w_bf[u][:, a:b, :]),
+                in0=by_rows(prob[u, a][:]),
+                in1=t_sb[:].unsqueeze(1).unsqueeze(3).to_broadcast([P, (b - a) // RUN, PACK, RUN]),
+                op=ALU.mult,
+            )
+
+        def quant_w(u):
+            quantise(w_codes[u][:], w_scales[u][:], w_bf[u][:])
+
+        def values(u):
+            h, c = units[u]
+            cols = slice(h * E, (h + 1) * E)
+            nc.tensor.matmul_mx(
+                out=y_banks[h][:, c, :],
+                lhsT=w_codes[u][:].bitcast(FP8X4),
+                lhsT_scale=w_scales[u][:],
+                rhs=v_codes[:, cols].bitcast(FP8X4),
+                rhs_scale=v_scales[:, cols],
+                start=True,
+                stop=True,
+            )
+
+        def invert(u):
+            h, c = units[u]
+            nc.vector.reciprocal(out=inverse[u][:], in_=y_banks[h][:, c, E - 1 : E])
+
+        def divide(u):
+            h, c = units[u]
+            rows = out[h, c * QC : (c + 1) * QC, :]
+            if last - 3 <= u < last:
+                nc.scalar.activation(out=result[u][:], in_=y_banks[h][:, c, :], func=ACT.Copy, scale=inverse[u][:])
+                queue = nc.scalar if u == last - 1 else nc.sync
+                queue.dma_start(out=rows, in_=result[u][:])
+            else:
+                nc.vector.tensor_scalar(
+                    out=result[u][:], in0=y_banks[h][:, c, :], scalar1=inverse[u][:], scalar2=None, op0=ALU.mult
+                )
+                nc.sync.dma_start(out=rows, in_=result[u][:])
+
+        pack_q(0)
+        pack_k(0)
+        quant_q(0)
+        for c in range(1, KP):
+            pack_k(c)
+        for r in range(PACK):
+            quant_k(r)
+            for u in range(H):
+                scores(u, r)
+        for r in range(2):
+            for u in range(H):
+                cap(u, r)
+        for u in range(H):
+            for r in range(2, PACK):
+                cap(u, r)
+        pack_q(1)
+        pack_v(0)
+        quant_q(1)
+        pack_v(1)
+        for u in range(2, 4):
+            for r in range(PACK):
+                scores(u, r)
+        pack_q(2)
+        quant_v()
+        quant_q(2)
+        for u in range(4, 6):
+            for r in range(PACK):
+                scores(u, r)
+
+        for u in range(last - 1):
+            exponentiate(u)
+            cap_all(u + 2)
+            weigh(u)
+            if u == 0:
+                pack_q(3)
+            else:
+                invert(u - 1)
+            quant_w(u)
+            if u == 0:
+                quant_q(3)
+                for later in range(6, 8):
+                    for r in range(PACK):
+                        scores(later, r)
+            values(u)
+            if 0 < u < last - 2:
+                divide(u - 1)
+        exponentiate(last - 1)
+        cap_all(last, 1)
+        exponentiate(last, 0)
+        exponentiate(last, 1)
+        weigh(last - 1)
+        invert(last - 2)
+        divide(last - 3)
+        divide(last - 2)
+        weigh(last, 0)
+        weigh(last, 1)
+        quant_w(last - 1)
+        values(last - 1)
+        quant_w(last)
+        values(last)
+        invert(last - 1)
+        invert(last)
+        divide(last - 1)
+        divide(last)

@@ -17,11 +17,9 @@ ALU = mybir.AluOpType
 P = 128
 PACK = 4
 ROWS = D // PACK
-QC = 128
-CHUNKS = NQ // QC
-KP = 4
-KW = N // KP
-RUN = 4
+QT = 128
+HALF = NQ // 2
+RUN = 2
 
 
 def tile_rows_kb_cap_kernel(tc, qT, kT, t, v, kb, out):
@@ -40,19 +38,17 @@ def tile_rows_kb_cap_kernel(tc, qT, kT, t, v, kb, out):
         kb_raw = tile("kb_raw", [P, PACK], F32)
         t_sb = tile("t_sb", [P, PACK], F32)
         kb_half = tile("kb_half", [P, PACK], F32)
-        q_raw = [tile("q_raw%d" % c, [P, PACK, QC], F32) for c in range(CHUNKS)]
-        k_raw = [tile("k_raw%d" % c, [P, PACK, KW], F32) for c in range(KP)]
+        q_raw = [tile("q_raw%d" % c, [P, PACK, HALF], F32) for c in range(2)]
+        k_raw = [tile("k_raw%d" % c, [P, 2, N], F32) for c in range(2)]
         v_raw = tile("v_raw", [P, H, PACK, E], F32)
 
+        nc.sync.dma_start(out=q_raw[0][:], in_=q_rows[:, :, 0:HALF])
         nc.scalar.dma_start(out=kb_raw[:], in_=kb.rearrange("(p r) o -> p (r o)", r=PACK))
         nc.scalar.dma_start(out=t_sb[:], in_=t.rearrange("(p r) o -> p (r o)", r=PACK))
-        nc.sync.dma_start(out=q_raw[0][:], in_=q_rows[:, :, 0:QC])
-        for c in range(KP):
-            nc.sync.dma_start(out=k_raw[c][:], in_=k_rows[:, :, c * KW : (c + 1) * KW])
-        nc.sync.dma_start(out=q_raw[1][:], in_=q_rows[:, :, QC : 2 * QC])
+        for c in range(2):
+            nc.sync.dma_start(out=k_raw[c][:], in_=k_rows[:, 2 * c : 2 * c + 2, :])
+        nc.sync.dma_start(out=q_raw[1][:], in_=q_rows[:, :, HALF:NQ])
         nc.sync.dma_start(out=v_raw[:], in_=v.rearrange("h (p r) e -> p h r e", r=PACK))
-        for c in range(2, CHUNKS):
-            nc.sync.dma_start(out=q_raw[c][:], in_=q_rows[:, :, c * QC : (c + 1) * QC])
 
         nc.scalar.mul(kb_half[:], kb_raw[:], 1.0 / CAP)
 
@@ -65,9 +61,9 @@ def tile_rows_kb_cap_kernel(tc, qT, kT, t, v, kb, out):
         def quantise(codes, scales, words):
             nc.vector.quantize_mx(out=codes.bitcast(FP8X4), scales=scales, in_=words.rearrange("p c j -> p (c j)"))
 
-        q_bf = [tile("q_bf%d" % c, [P, QC, PACK], BF16) for c in range(CHUNKS)]
-        q_codes = [tile("q_codes%d" % c, [P, QC], U32) for c in range(CHUNKS)]
-        q_scales = [tile("q_scales%d" % c, [P, QC], U8) for c in range(CHUNKS)]
+        q_bf = [tile("q_bf%d" % c, [P, HALF, PACK], BF16) for c in range(2)]
+        q_codes = [tile("q_codes%d" % c, [P, HALF], U32) for c in range(2)]
+        q_scales = [tile("q_scales%d" % c, [P, HALF], U8) for c in range(2)]
         k_bf = tile("k_bf", [P, PACK, P, PACK], BF16)
         k_codes = [tile("k_codes%d" % r, [P, P], U32) for r in range(PACK)]
         k_scales = [tile("k_scales%d" % r, [P, P], U8) for r in range(PACK)]
@@ -81,11 +77,10 @@ def tile_rows_kb_cap_kernel(tc, qT, kT, t, v, kb, out):
         def quant_q(c):
             quantise(q_codes[c][:], q_scales[c][:], q_bf[c][:])
 
-        def pack_k(c):
-            places = KW // PACK
+        def pack_k(c, r0, r1):
             nc.vector.tensor_copy(
-                out=k_bf[:, :, c * places : (c + 1) * places, :].rearrange("p r s j -> p s j r"),
-                in_=k_raw[c][:].rearrange("p j (s r) -> p s j r", r=PACK),
+                out=k_bf[:, r0:r1, :, 2 * c : 2 * c + 2].rearrange("p r s j -> p s j r"),
+                in_=k_raw[c][:].rearrange("p j (s r) -> p s j r", r=PACK)[:, :, :, r0:r1],
             )
 
         def quant_k(r):
@@ -97,58 +92,54 @@ def tile_rows_kb_cap_kernel(tc, qT, kT, t, v, kb, out):
         def quant_v():
             quantise(v_codes[:], v_scales[:], v_bf[:])
 
-        units = [(h, c) for c in range(CHUNKS) for h in range(H)]
+        units = [(h, c, x) for c in range(2) for h in range(H) for x in range(2)]
         last = len(units) - 1
-        score_banks = [[ps.tile([P, PACK, QC], F32, name="score%d_%d" % (h, b)) for b in range(3)] for h in range(H)]
-        y_banks = [ps.tile([P, CHUNKS, E], F32, name="y%d" % h) for h in range(H)]
+        score_banks = [[ps.tile([P, 2, HALF], F32, name="score%d_%d" % (h, b)) for b in range(3 - h)] for h in range(H)]
+        y_banks = [ps.tile([P, 4, E], F32, name="y%d" % b) for b in range(3)]
 
-        def score_place(u, r):
-            h, c = units[u]
-            bank = min(r, 2) if c == 0 else c - 1
-            return score_banks[h][bank][:, r, :]
+        def score_place(h, c, r):
+            bank = min(r, 2) if (h, c) == (0, 0) else r // 2
+            return score_banks[h][bank][:, r % 2, :]
 
-        def scores(u, r):
-            h, c = units[u]
+        def scores(h, c, r):
             rows = slice(h * ROWS, (h + 1) * ROWS)
-            nc.tensor.matmul_mx(
-                out=score_place(u, r),
-                lhsT=k_codes[r][rows, :].bitcast(FP8X4),
-                lhsT_scale=k_scales[r][rows, :],
-                rhs=q_codes[c][rows, :].bitcast(FP8X4),
-                rhs_scale=q_scales[c][rows, :],
-                start=True,
-                stop=True,
-            )
+            for x in range(2):
+                cols = slice(x * QT, (x + 1) * QT)
+                nc.tensor.matmul_mx(
+                    out=score_place(h, c, r)[:, cols],
+                    lhsT=k_codes[r][rows, :].bitcast(FP8X4),
+                    lhsT_scale=k_scales[r][rows, :],
+                    rhs=q_codes[c][rows, cols].bitcast(FP8X4),
+                    rhs_scale=q_scales[c][rows, cols],
+                    start=True,
+                    stop=True,
+                )
 
         def pieces(u):
-            return [(0, QC // 2), (QC // 2, QC)] if u == last else [(0, QC)]
+            return [(0, QT // 2), (QT // 2, QT)] if u == last else [(0, QT)]
 
-        capped = {}
-        prob = {}
-        for u in range(len(units)):
-            for a, b in pieces(u):
-                capped[u, a] = tile("capped%d_%d" % (u, a), [P, PACK, b - a], F32)
-                prob[u, a] = tile("prob%d_%d" % (u, a), [P, PACK, b - a], F32)
-        w_bf = [tile("w_bf%d" % u, [P, QC, PACK], BF16) for u in range(len(units))]
-        w_codes = [tile("w_codes%d" % u, [P, QC], U32) for u in range(len(units))]
-        w_scales = [tile("w_scales%d" % u, [P, QC], U8) for u in range(len(units))]
+        capped = {(h, c): tile("capped%d_%d" % (h, c), [P, PACK, HALF], F32) for h in range(H) for c in range(2)}
+        prob = {
+            (u, a): tile("prob%d_%d" % (u, a), [P, PACK, b - a], F32) for u in range(len(units)) for a, b in pieces(u)
+        }
+        w_bf = [tile("w_bf%d" % u, [P, QT, PACK], BF16) for u in range(len(units))]
+        w_codes = [tile("w_codes%d" % u, [P, QT], U32) for u in range(len(units))]
+        w_scales = [tile("w_scales%d" % u, [P, QT], U8) for u in range(len(units))]
         inverse = [tile("inverse%d" % u, [P, 1], F32) for u in range(len(units))]
         result = [tile("result%d" % u, [P, E], F32) for u in range(len(units))]
 
-        def cap(u, r, piece=0):
-            a, b = pieces(u)[piece]
+        def cap(h, c, r):
             nc.scalar.activation(
-                out=capped[u, a][:, r, :], in_=score_place(u, r)[:, a:b], func=ACT.Tanh,
+                out=capped[h, c][:, r, :], in_=score_place(h, c, r), func=ACT.Tanh,
                 bias=kb_half[:, r : r + 1], scale=1.0 / CAP,
             )
 
-        def cap_all(u, piece=0):
-            for r in range(PACK):
-                cap(u, r, piece)
-
         def exponentiate(u, piece=0):
+            h, c, x = units[u]
             a, b = pieces(u)[piece]
-            nc.scalar.activation(out=prob[u, a][:], in_=capped[u, a][:], func=ACT.Exp, scale=CAP)
+            nc.scalar.activation(
+                out=prob[u, a][:], in_=capped[h, c][:, :, x * QT + a : x * QT + b], func=ACT.Exp, scale=CAP
+            )
 
         def weigh(u, piece=0):
             a, b = pieces(u)[piece]
@@ -162,11 +153,14 @@ def tile_rows_kb_cap_kernel(tc, qT, kT, t, v, kb, out):
         def quant_w(u):
             quantise(w_codes[u][:], w_scales[u][:], w_bf[u][:])
 
+        def y_place(u):
+            return y_banks[u % 3][:, u // 3, :]
+
         def values(u):
-            h, c = units[u]
+            h = units[u][0]
             cols = slice(h * E, (h + 1) * E)
             nc.tensor.matmul_mx(
-                out=y_banks[h][:, c, :],
+                out=y_place(u),
                 lhsT=w_codes[u][:].bitcast(FP8X4),
                 lhsT_scale=w_scales[u][:],
                 rhs=v_codes[:, cols].bitcast(FP8X4),
@@ -176,80 +170,84 @@ def tile_rows_kb_cap_kernel(tc, qT, kT, t, v, kb, out):
             )
 
         def invert(u):
-            h, c = units[u]
-            nc.vector.reciprocal(out=inverse[u][:], in_=y_banks[h][:, c, E - 1 : E])
+            nc.vector.reciprocal(out=inverse[u][:], in_=y_place(u)[:, E - 1 : E])
 
         def divide(u):
-            h, c = units[u]
-            rows = out[h, c * QC : (c + 1) * QC, :]
-            if last - 3 <= u < last:
-                nc.scalar.activation(out=result[u][:], in_=y_banks[h][:, c, :], func=ACT.Copy, scale=inverse[u][:])
+            h, c, x = units[u]
+            first = c * HALF + x * QT
+            rows = out[h, first : first + QT, :]
+            if last - 4 <= u < last:
+                nc.scalar.activation(out=result[u][:], in_=y_place(u), func=ACT.Copy, scale=inverse[u][:])
                 queue = nc.scalar if u == last - 1 else nc.sync
                 queue.dma_start(out=rows, in_=result[u][:])
             else:
                 nc.vector.tensor_scalar(
-                    out=result[u][:], in0=y_banks[h][:, c, :], scalar1=inverse[u][:], scalar2=None, op0=ALU.mult
+                    out=result[u][:], in0=y_place(u), scalar1=inverse[u][:], scalar2=None, op0=ALU.mult
                 )
                 nc.sync.dma_start(out=rows, in_=result[u][:])
 
         pack_q(0)
-        pack_k(0)
+        pack_k(0, 0, 2)
         quant_q(0)
-        for c in range(1, KP):
-            pack_k(c)
-        for r in range(PACK):
-            quant_k(r)
-            for u in range(H):
-                scores(u, r)
-        for r in range(2):
-            for u in range(H):
-                cap(u, r)
-        for u in range(H):
-            for r in range(2, PACK):
-                cap(u, r)
+        pack_k(0, 2, 4)
+        pack_k(1, 0, 1)
+        pack_k(1, 1, 2)
+        quant_k(0)
+        scores(0, 0, 0)
+        scores(1, 0, 0)
+        cap(0, 0, 0)
+        pack_k(1, 2, 4)
+        quant_k(1)
+        scores(0, 0, 1)
+        scores(1, 0, 1)
+        cap(0, 0, 1)
+        cap(1, 0, 0)
+        cap(1, 0, 1)
+        quant_k(2)
+        quant_k(3)
+        for h in range(H):
+            for r in (2, 3):
+                scores(h, 0, r)
+            for r in (2, 3):
+                cap(h, 0, r)
         pack_q(1)
         pack_v(0)
         quant_q(1)
         pack_v(1)
-        for u in range(2, 4):
+        for h in range(H):
             for r in range(PACK):
-                scores(u, r)
-        pack_q(2)
+                scores(h, 1, r)
         quant_v()
-        quant_q(2)
-        for u in range(4, 6):
-            for r in range(PACK):
-                scores(u, r)
 
-        for u in range(last - 1):
+        caps_after = {0: [(0, 0), (0, 1)], 1: [(0, 2), (0, 3)], 2: [(1, 0)], 3: [(1, 1)], 4: [(1, 2), (1, 3)]}
+        for u in range(last - 2):
             exponentiate(u)
-            cap_all(u + 2)
+            for h, r in caps_after[u]:
+                cap(h, 1, r)
             weigh(u)
-            if u == 0:
-                pack_q(3)
-            else:
+            if u > 0:
                 invert(u - 1)
             quant_w(u)
-            if u == 0:
-                quant_q(3)
-                for later in range(6, 8):
-                    for r in range(PACK):
-                        scores(later, r)
             values(u)
-            if 0 < u < last - 2:
+            if 0 < u < last - 3:
                 divide(u - 1)
+        exponentiate(last - 2)
         exponentiate(last - 1)
-        cap_all(last, 1)
         exponentiate(last, 0)
         exponentiate(last, 1)
-        weigh(last - 1)
-        invert(last - 2)
+        weigh(last - 2)
+        invert(last - 3)
+        divide(last - 4)
         divide(last - 3)
-        divide(last - 2)
+        weigh(last - 1)
+        quant_w(last - 2)
+        values(last - 2)
         weigh(last, 0)
         weigh(last, 1)
         quant_w(last - 1)
         values(last - 1)
+        invert(last - 2)
+        divide(last - 2)
         quant_w(last)
         values(last)
         invert(last - 1)

@@ -89,8 +89,9 @@ def tile_rows_kb_cap_kernel(tc, qT, kT, t, v, kb, out):
         def pack_v(h):
             nc.vector.tensor_copy(out=side_by_side(v_bf[:, h * E : (h + 1) * E, :]), in_=by_rows(v_raw[:, h, :, :]))
 
-        def quant_v():
-            quantise(v_codes[:], v_scales[:], v_bf[:])
+        def quant_v(h):
+            cols = slice(h * E, (h + 1) * E)
+            quantise(v_codes[:, cols], v_scales[:, cols], v_bf[:, cols, :])
 
         units = [(h, c, x) for c in range(2) for h in range(H) for x in range(2)]
         last = len(units) - 1
@@ -116,7 +117,7 @@ def tile_rows_kb_cap_kernel(tc, qT, kT, t, v, kb, out):
                 )
 
         def pieces(u):
-            return [(0, QT // 2), (QT // 2, QT)] if u == last else [(0, QT)]
+            return [(0, QT)]
 
         capped = {(h, c): tile("capped%d_%d" % (h, c), [P, PACK, HALF], F32) for h in range(H) for c in range(2)}
         prob = {
@@ -208,49 +209,45 @@ def tile_rows_kb_cap_kernel(tc, qT, kT, t, v, kb, out):
         for h in range(H):
             for r in (2, 3):
                 scores(h, 0, r)
-            for r in (2, 3):
-                cap(h, 0, r)
+        cap(0, 0, 2)
+        cap(0, 0, 3)
+        cap(1, 0, 2)
+        exponentiate(0)
+        cap(1, 0, 3)
         pack_q(1)
-        pack_v(0)
         quant_q(1)
-        pack_v(1)
         for h in range(H):
             for r in range(PACK):
                 scores(h, 1, r)
-        quant_v()
+        pack_v(0)
+        pack_v(1)
+        quant_v(0)
 
-        caps_after = {0: [(0, 0), (0, 1)], 1: [(0, 2), (0, 3)], 2: [(1, 0)], 3: [(1, 1)], 4: [(1, 2), (1, 3)]}
         for u in range(last - 2):
-            exponentiate(u)
-            for h, r in caps_after[u]:
-                cap(h, 1, r)
+            exponentiate(u + 1)
+            if u < 4:
+                for r in (2 * (u % 2), 2 * (u % 2) + 1):
+                    cap(u // 2, 1, r)
             weigh(u)
+            if u == 0:
+                quant_v(1)
             if u > 0:
                 invert(u - 1)
+            if u > 1:
+                divide(u - 2)
             quant_w(u)
             values(u)
-            if 0 < u < last - 3:
-                divide(u - 1)
-        exponentiate(last - 2)
         exponentiate(last - 1)
-        exponentiate(last, 0)
-        exponentiate(last, 1)
+        exponentiate(last)
+        divide(last - 4)
         weigh(last - 2)
         invert(last - 3)
-        divide(last - 4)
         divide(last - 3)
         weigh(last - 1)
-        quant_w(last - 2)
-        values(last - 2)
-        weigh(last, 0)
-        weigh(last, 1)
-        quant_w(last - 1)
-        values(last - 1)
-        invert(last - 2)
-        divide(last - 2)
-        quant_w(last)
-        values(last)
-        invert(last - 1)
-        invert(last)
-        divide(last - 1)
-        divide(last)
+        weigh(last)
+        for u in range(last - 2, last + 1):
+            quant_w(u)
+            values(u)
+        for u in range(last - 2, last + 1):
+            invert(u)
+            divide(u)

@@ -18,8 +18,17 @@ P = 128
 PACK = 4
 ROWS = D // PACK
 QT = 128
-HALF = NQ // 2
 RUN = 2
+
+Q_LOADS = [(0, 1), (1, 3), (3, 4)]
+SPANS = [[(0, 1), (1, 4)], [(0, 1), (1, 3), (3, 4)]]
+UNITS = [(h, c, x) for h, c in ((0, 0), (1, 0), (1, 1), (0, 1), (1, 2)) for x in range(*SPANS[h][c])]
+LAST = len(UNITS) - 1
+SCORE_BANKS = [3, 2]
+FIRST_SPAN_BANK = [[0, 1, 2, 0], [0, 1, 1, 0]]
+Y_PLACES = [(0, 0), (0, 1), (1, 0), (1, 1), (2, 0), (2, 1), (0, 2), (1, 2)]
+Y_BANKS, Y_SLOTS = 3, 4
+SCALAR_DIVIDES = range(2, LAST)
 
 
 def tile_rows_kb_cap_kernel(tc, qT, kT, t, v, kb, out):
@@ -32,25 +41,61 @@ def tile_rows_kb_cap_kernel(tc, qT, kT, t, v, kb, out):
         def tile(name, shape, dtype):
             return sb.tile(shape, dtype, name=name, align_bytes=64)
 
+        q_widths = [(end - first) * QT for first, end in Q_LOADS]
+        kb_raw = tile("kb_raw", [P, PACK], F32)
+        t_sb = tile("t_sb", [P, PACK], F32)
+        kb_over_cap = tile("kb_over_cap", [P, PACK], F32)
+        q_raw = [tile("q_raw%d" % g, [P, PACK, width], F32) for g, width in enumerate(q_widths)]
+        k_raw = [tile("k_raw%d" % g, [P, 2, N], F32) for g in range(2)]
+        v_raw = tile("v_raw", [P, H, PACK, E], F32)
+
         q_rows = qT.rearrange("h (p j) n -> (h p) j n", j=PACK)
         k_rows = kT.rearrange("h (p j) n -> (h p) j n", j=PACK)
 
-        kb_raw = tile("kb_raw", [P, PACK], F32)
-        t_sb = tile("t_sb", [P, PACK], F32)
-        kb_half = tile("kb_half", [P, PACK], F32)
-        q_raw = [tile("q_raw%d" % c, [P, PACK, HALF], F32) for c in range(2)]
-        k_raw = [tile("k_raw%d" % c, [P, 2, N], F32) for c in range(2)]
-        v_raw = tile("v_raw", [P, H, PACK, E], F32)
+        def load_q(g):
+            first, end = Q_LOADS[g]
+            nc.sync.dma_start(out=q_raw[g][:], in_=q_rows[:, :, first * QT : end * QT])
 
-        nc.sync.dma_start(out=q_raw[0][:], in_=q_rows[:, :, 0:HALF])
-        nc.scalar.dma_start(out=kb_raw[:], in_=kb.rearrange("(p r) o -> p (r o)", r=PACK))
-        nc.scalar.dma_start(out=t_sb[:], in_=t.rearrange("(p r) o -> p (r o)", r=PACK))
-        for c in range(2):
-            nc.sync.dma_start(out=k_raw[c][:], in_=k_rows[:, 2 * c : 2 * c + 2, :])
-        nc.sync.dma_start(out=q_raw[1][:], in_=q_rows[:, :, HALF:NQ])
-        nc.sync.dma_start(out=v_raw[:], in_=v.rearrange("h (p r) e -> p h r e", r=PACK))
+        load_q(0)
+        for g in range(2):
+            nc.sync.dma_start(out=k_raw[g][:], in_=k_rows[:, 2 * g : 2 * g + 2, :])
+        nc.sync.dma_start(out=kb_raw[:], in_=kb.rearrange("(s r) o -> s (r o)", r=PACK))
+        nc.sync.dma_start(out=t_sb[:], in_=t.rearrange("(s r) o -> s (r o)", r=PACK))
+        load_q(1)
+        load_q(2)
+        nc.sync.dma_start(out=v_raw[:], in_=v.rearrange("h (s r) e -> s h r e", r=PACK))
 
-        nc.scalar.mul(kb_half[:], kb_raw[:], 1.0 / CAP)
+        q_bf = [tile("q_bf%d" % g, [P, width, PACK], BF16) for g, width in enumerate(q_widths)]
+        q_codes = [tile("q_codes%d" % g, [P, width], U32) for g, width in enumerate(q_widths)]
+        q_scales = [tile("q_scales%d" % g, [P, width], U8) for g, width in enumerate(q_widths)]
+        k_bf = tile("k_bf", [P, PACK, P, PACK], BF16)
+        k_codes = [tile("k_codes%d" % r, [P, P], U32) for r in range(PACK)]
+        k_scales = [tile("k_scales%d" % r, [P, P], U8) for r in range(PACK)]
+        v_bf = tile("v_bf", [P, H * E, PACK], BF16)
+        v_codes = tile("v_codes", [P, H * E], U32)
+        v_scales = tile("v_scales", [P, H * E], U8)
+
+        score_banks = [
+            [ps.tile([P, NQ], F32, name="score%d_%d" % (h, b)) for b in range(SCORE_BANKS[h])] for h in range(H)
+        ]
+        y_banks = [ps.tile([P, Y_SLOTS, E], F32, name="y%d" % b) for b in range(Y_BANKS)]
+
+        def pieces(u):
+            return [(0, QT // 2), (QT // 2, QT)] if u == LAST else [(0, QT)]
+
+        capped = {
+            (h, c): tile("capped%d_%d" % (h, c), [P, PACK, (end - first) * QT], F32)
+            for h in range(H)
+            for c, (first, end) in enumerate(SPANS[h])
+        }
+        prob = {
+            (u, a): tile("prob%d_%d" % (u, a), [P, PACK, b - a], F32) for u in range(len(UNITS)) for a, b in pieces(u)
+        }
+        w_bf = tile("w_bf", [P, len(UNITS) * QT, PACK], BF16)
+        w_codes = tile("w_codes", [P, len(UNITS) * QT], U32)
+        w_scales = tile("w_scales", [P, len(UNITS) * QT], U8)
+        inverse = tile("inverse", [P, len(UNITS)], F32)
+        result = [tile("result%d" % u, [P, E], F32) for u in range(len(UNITS))]
 
         def side_by_side(words):
             return words.rearrange("p (c i) j -> p c j i", i=RUN)
@@ -61,193 +106,202 @@ def tile_rows_kb_cap_kernel(tc, qT, kT, t, v, kb, out):
         def quantise(codes, scales, words):
             nc.vector.quantize_mx(out=codes.bitcast(FP8X4), scales=scales, in_=words.rearrange("p c j -> p (c j)"))
 
-        q_bf = [tile("q_bf%d" % c, [P, HALF, PACK], BF16) for c in range(2)]
-        q_codes = [tile("q_codes%d" % c, [P, HALF], U32) for c in range(2)]
-        q_scales = [tile("q_scales%d" % c, [P, HALF], U8) for c in range(2)]
-        k_bf = tile("k_bf", [P, PACK, P, PACK], BF16)
-        k_codes = [tile("k_codes%d" % r, [P, P], U32) for r in range(PACK)]
-        k_scales = [tile("k_scales%d" % r, [P, P], U8) for r in range(PACK)]
-        v_bf = tile("v_bf", [P, H * E, PACK], BF16)
-        v_codes = tile("v_codes", [P, H * E], U32)
-        v_scales = tile("v_scales", [P, H * E], U8)
+        def prepare_q(g):
+            nc.vector.tensor_copy(out=side_by_side(q_bf[g][:]), in_=by_rows(q_raw[g][:]))
+            quantise(q_codes[g][:], q_scales[g][:], q_bf[g][:])
 
-        def pack_q(c):
-            nc.vector.tensor_copy(out=side_by_side(q_bf[c][:]), in_=by_rows(q_raw[c][:]))
+        def k_views(g, r0, r1):
+            words = k_bf[:, r0:r1, :, 2 * g : 2 * g + 2].rearrange("p r s j -> p s j r")
+            rows = k_raw[g][:].rearrange("p j (s r) -> p s j r", r=PACK)[:, :, :, r0:r1]
+            return words, rows
 
-        def quant_q(c):
-            quantise(q_codes[c][:], q_scales[c][:], q_bf[c][:])
+        def pack_k(g, r0, r1):
+            words, rows = k_views(g, r0, r1)
+            nc.vector.tensor_copy(out=words, in_=rows)
 
-        def pack_k(c, r0, r1):
-            nc.vector.tensor_copy(
-                out=k_bf[:, r0:r1, :, 2 * c : 2 * c + 2].rearrange("p r s j -> p s j r"),
-                in_=k_raw[c][:].rearrange("p j (s r) -> p s j r", r=PACK)[:, :, :, r0:r1],
-            )
+        def pack_k_on_scalar(g, r0, r1):
+            words, rows = k_views(g, r0, r1)
+            nc.scalar.activation(out=words, in_=rows, func=ACT.Copy)
 
-        def quant_k(r):
+        def quantise_k(r):
             quantise(k_codes[r][:], k_scales[r][:], k_bf[:, r, :, :])
 
         def pack_v(h):
             nc.vector.tensor_copy(out=side_by_side(v_bf[:, h * E : (h + 1) * E, :]), in_=by_rows(v_raw[:, h, :, :]))
 
-        def quant_v(h):
-            cols = slice(h * E, (h + 1) * E)
-            quantise(v_codes[:, cols], v_scales[:, cols], v_bf[:, cols, :])
-
-        units = [(h, c, x) for c in range(2) for h in range(H) for x in range(2)]
-        last = len(units) - 1
-        score_banks = [[ps.tile([P, 2, HALF], F32, name="score%d_%d" % (h, b)) for b in range(3 - h)] for h in range(H)]
-        y_banks = [ps.tile([P, 4, E], F32, name="y%d" % b) for b in range(3)]
-
         def score_place(h, c, r):
-            bank = min(r, 2) if (h, c) == (0, 0) else r // 2
-            return score_banks[h][bank][:, r % 2, :]
+            first, end = SPANS[h][c]
+            width = (end - first) * QT
+            per_bank = NQ // width
+            if c == 0:
+                bank, slot = FIRST_SPAN_BANK[h][r], r
+            elif per_bank == 1:
+                bank, slot = (r + 1) % SCORE_BANKS[h], 0
+            else:
+                bank, slot = divmod(r, per_bank)
+            return score_banks[h][bank][:, slot * width : (slot + 1) * width]
 
         def scores(h, c, r):
             rows = slice(h * ROWS, (h + 1) * ROWS)
-            for x in range(2):
-                cols = slice(x * QT, (x + 1) * QT)
+            first, end = SPANS[h][c]
+            for x in range(first, end):
+                g = [i for i, (a, b) in enumerate(Q_LOADS) if a <= x < b][0]
+                cols = slice((x - Q_LOADS[g][0]) * QT, (x - Q_LOADS[g][0] + 1) * QT)
                 nc.tensor.matmul_mx(
-                    out=score_place(h, c, r)[:, cols],
+                    out=score_place(h, c, r)[:, (x - first) * QT : (x - first + 1) * QT],
                     lhsT=k_codes[r][rows, :].bitcast(FP8X4),
                     lhsT_scale=k_scales[r][rows, :],
-                    rhs=q_codes[c][rows, cols].bitcast(FP8X4),
-                    rhs_scale=q_scales[c][rows, cols],
+                    rhs=q_codes[g][rows, cols].bitcast(FP8X4),
+                    rhs_scale=q_scales[g][rows, cols],
                     start=True,
                     stop=True,
                 )
 
-        def pieces(u):
-            return [(0, QT)]
-
-        capped = {(h, c): tile("capped%d_%d" % (h, c), [P, PACK, HALF], F32) for h in range(H) for c in range(2)}
-        prob = {
-            (u, a): tile("prob%d_%d" % (u, a), [P, PACK, b - a], F32) for u in range(len(units)) for a, b in pieces(u)
-        }
-        w_bf = [tile("w_bf%d" % u, [P, QT, PACK], BF16) for u in range(len(units))]
-        w_codes = [tile("w_codes%d" % u, [P, QT], U32) for u in range(len(units))]
-        w_scales = [tile("w_scales%d" % u, [P, QT], U8) for u in range(len(units))]
-        inverse = [tile("inverse%d" % u, [P, 1], F32) for u in range(len(units))]
-        result = [tile("result%d" % u, [P, E], F32) for u in range(len(units))]
-
         def cap(h, c, r):
             nc.scalar.activation(
-                out=capped[h, c][:, r, :], in_=score_place(h, c, r), func=ACT.Tanh,
-                bias=kb_half[:, r : r + 1], scale=1.0 / CAP,
+                out=capped[h, c][:, r, :],
+                in_=score_place(h, c, r),
+                func=ACT.Tanh,
+                bias=kb_over_cap[:, r : r + 1],
+                scale=1.0 / CAP,
             )
 
         def exponentiate(u, piece=0):
-            h, c, x = units[u]
+            h, c, x = UNITS[u]
             a, b = pieces(u)[piece]
+            start = (x - SPANS[h][c][0]) * QT
             nc.scalar.activation(
-                out=prob[u, a][:], in_=capped[h, c][:, :, x * QT + a : x * QT + b], func=ACT.Exp, scale=CAP
+                out=prob[u, a][:], in_=capped[h, c][:, :, start + a : start + b], func=ACT.Exp, scale=CAP
             )
 
         def weigh(u, piece=0):
             a, b = pieces(u)[piece]
             nc.vector.tensor_tensor(
-                out=side_by_side(w_bf[u][:, a:b, :]),
+                out=side_by_side(w_bf[:, u * QT + a : u * QT + b, :]),
                 in0=by_rows(prob[u, a][:]),
                 in1=t_sb[:].unsqueeze(1).unsqueeze(3).to_broadcast([P, (b - a) // RUN, PACK, RUN]),
                 op=ALU.mult,
             )
 
-        def quant_w(u):
-            quantise(w_codes[u][:], w_scales[u][:], w_bf[u][:])
+        def quantise_w(u, count=1):
+            cols = slice(u * QT, (u + count) * QT)
+            quantise(w_codes[:, cols], w_scales[:, cols], w_bf[:, cols, :])
 
         def y_place(u):
-            return y_banks[u % 3][:, u // 3, :]
+            bank, slot = Y_PLACES[u]
+            return y_banks[bank][:, slot, :]
 
         def values(u):
-            h = units[u][0]
+            h = UNITS[u][0]
+            queries = slice(u * QT, (u + 1) * QT)
             cols = slice(h * E, (h + 1) * E)
             nc.tensor.matmul_mx(
                 out=y_place(u),
-                lhsT=w_codes[u][:].bitcast(FP8X4),
-                lhsT_scale=w_scales[u][:],
+                lhsT=w_codes[:, queries].bitcast(FP8X4),
+                lhsT_scale=w_scales[:, queries],
                 rhs=v_codes[:, cols].bitcast(FP8X4),
                 rhs_scale=v_scales[:, cols],
                 start=True,
                 stop=True,
             )
 
-        def invert(u):
-            nc.vector.reciprocal(out=inverse[u][:], in_=y_place(u)[:, E - 1 : E])
+        def quantise_and_multiply(u):
+            quantise_w(u)
+            values(u)
+
+        def invert(u, count=1):
+            bank, slot = Y_PLACES[u]
+            nc.vector.reciprocal(out=inverse[:, u : u + count], in_=y_banks[bank][:, slot : slot + count, E - 1])
 
         def divide(u):
-            h, c, x = units[u]
-            first = c * HALF + x * QT
-            rows = out[h, first : first + QT, :]
-            if last - 4 <= u < last:
-                nc.scalar.activation(out=result[u][:], in_=y_place(u), func=ACT.Copy, scale=inverse[u][:])
-                queue = nc.scalar if u == last - 1 else nc.sync
-                queue.dma_start(out=rows, in_=result[u][:])
+            h, c, x = UNITS[u]
+            if u in SCALAR_DIVIDES:
+                nc.scalar.activation(out=result[u][:], in_=y_place(u), func=ACT.Copy, scale=inverse[:, u : u + 1])
             else:
                 nc.vector.tensor_scalar(
-                    out=result[u][:], in0=y_place(u), scalar1=inverse[u][:], scalar2=None, op0=ALU.mult
+                    out=result[u][:], in0=y_place(u), scalar1=inverse[:, u : u + 1], scalar2=None, op0=ALU.mult
                 )
-                nc.sync.dma_start(out=rows, in_=result[u][:])
+            queue = nc.scalar if u == LAST - 1 else nc.sync
+            queue.dma_start(out=out[h, x * QT : (x + 1) * QT, :], in_=result[u][:])
 
-        pack_q(0)
+        prepare_q(0)
         pack_k(0, 0, 2)
-        quant_q(0)
         pack_k(0, 2, 4)
         pack_k(1, 0, 1)
         pack_k(1, 1, 2)
-        quant_k(0)
-        scores(0, 0, 0)
-        scores(1, 0, 0)
-        cap(0, 0, 0)
-        pack_k(1, 2, 4)
-        quant_k(1)
-        scores(0, 0, 1)
-        scores(1, 0, 1)
-        cap(0, 0, 1)
-        cap(1, 0, 0)
-        cap(1, 0, 1)
-        quant_k(2)
-        quant_k(3)
-        for h in range(H):
-            for r in (2, 3):
+        pack_k_on_scalar(1, 2, 4)
+        nc.scalar.mul(kb_over_cap[:], kb_raw[:], 1.0 / CAP)
+        for r, heads in ((0, (0, 1)), (1, (1, 0))):
+            quantise_k(r)
+            for h in heads:
                 scores(h, 0, r)
-        cap(0, 0, 2)
-        cap(0, 0, 3)
-        cap(1, 0, 2)
+            for h in heads:
+                cap(h, 0, r)
+        quantise_k(2)
+        quantise_k(3)
+        rest_of_first_span = ((0, 2), (0, 3), (1, 3), (1, 2))
+        for h, r in rest_of_first_span:
+            scores(h, 0, r)
+        for h, r in rest_of_first_span:
+            cap(h, 0, r)
         exponentiate(0)
-        cap(1, 0, 3)
-        pack_q(1)
-        quant_q(1)
-        for h in range(H):
-            for r in range(PACK):
-                scores(h, 1, r)
-        pack_v(0)
-        pack_v(1)
-        quant_v(0)
+        exponentiate(1)
 
-        for u in range(last - 2):
-            exponentiate(u + 1)
-            if u < 4:
-                for r in (2 * (u % 2), 2 * (u % 2) + 1):
-                    cap(u // 2, 1, r)
-            weigh(u)
-            if u == 0:
-                quant_v(1)
-            if u > 0:
-                invert(u - 1)
-            if u > 1:
-                divide(u - 2)
-            quant_w(u)
-            values(u)
-        exponentiate(last - 1)
-        exponentiate(last)
-        divide(last - 4)
-        weigh(last - 2)
-        invert(last - 3)
-        divide(last - 3)
-        weigh(last - 1)
-        weigh(last)
-        for u in range(last - 2, last + 1):
-            quant_w(u)
-            values(u)
-        for u in range(last - 2, last + 1):
+        prepare_q(1)
+        prepare_q(2)
+        for r in range(PACK):
+            scores(1, 1, r)
+        for r in range(SCORE_BANKS[0]):
+            scores(0, 1, r)
+        for r in range(PACK):
+            cap(1, 1, r)
+        for r in range(PACK):
+            scores(1, 2, r)
+        cap(0, 1, 0)
+        scores(0, 1, 3)
+        for h in range(H):
+            weigh(h)
+            pack_v(h)
+        quantise_w(0, 2)
+        quantise(v_codes[:], v_scales[:], v_bf[:])
+        values(0)
+        values(1)
+
+        exponentiate(2)
+        cap(0, 1, 1)
+        exponentiate(3)
+        cap(0, 1, 2)
+        cap(0, 1, 3)
+        cap(1, 2, 0)
+        for u in (4, 5, 6):
+            exponentiate(u)
+        for r in range(1, PACK):
+            cap(1, 2, r)
+
+        weigh(2)
+        invert(0, 2)
+        quantise_and_multiply(2)
+        weigh(3)
+        divide(0)
+        divide(1)
+        quantise_and_multiply(3)
+        weigh(4)
+        invert(2, 2)
+        divide(2)
+        exponentiate(LAST, 0)
+        exponentiate(LAST, 1)
+        divide(3)
+        weigh(5)
+        quantise_and_multiply(4)
+        weigh(6)
+        quantise_and_multiply(5)
+        weigh(LAST, 0)
+        weigh(LAST, 1)
+        quantise_and_multiply(6)
+        invert(4, 2)
+        quantise_and_multiply(LAST)
+        divide(4)
+        divide(5)
+        for u in (LAST - 1, LAST):
             invert(u)
             divide(u)

@@ -22,13 +22,13 @@ RUN = 2
 
 Q_LOADS = [(0, 1), (1, 3), (3, 4)]
 SPANS = [[(0, 1), (1, 4)], [(0, 1), (1, 3), (3, 4)]]
-UNITS = [(h, c, x) for h, c in ((0, 0), (1, 0), (1, 1), (0, 1), (1, 2)) for x in range(*SPANS[h][c])]
+UNITS = [(h, c, x) for h, c in ((0, 0), (1, 0), (0, 1), (1, 1), (1, 2)) for x in range(*SPANS[h][c])]
 LAST = len(UNITS) - 1
 SCORE_BANKS = [3, 2]
-FIRST_SPAN_BANK = [[0, 1, 2, 0], [0, 1, 1, 0]]
-Y_PLACES = [(0, 0), (0, 1), (1, 0), (1, 1), (2, 0), (2, 1), (0, 2), (1, 2)]
+Y_PLACES = [(0, 0), (1, 0), (0, 1), (0, 2), (2, 0), (2, 1), (0, 3), (1, 1)]
 Y_BANKS, Y_SLOTS = 3, 4
 SCALAR_DIVIDES = range(2, LAST)
+PIECES = [1, 1, 1, 1, 1, 1, 2, 2]
 
 
 def tile_rows_kb_cap_kernel(tc, qT, kT, t, v, kb, out):
@@ -60,10 +60,10 @@ def tile_rows_kb_cap_kernel(tc, qT, kT, t, v, kb, out):
         for g in range(2):
             nc.sync.dma_start(out=k_raw[g][:], in_=k_rows[:, 2 * g : 2 * g + 2, :])
         nc.sync.dma_start(out=kb_raw[:], in_=kb.rearrange("(s r) o -> s (r o)", r=PACK))
-        nc.sync.dma_start(out=t_sb[:], in_=t.rearrange("(s r) o -> s (r o)", r=PACK))
         load_q(1)
         load_q(2)
         nc.sync.dma_start(out=v_raw[:], in_=v.rearrange("h (s r) e -> s h r e", r=PACK))
+        nc.sync.dma_start(out=t_sb[:], in_=t.rearrange("(s r) o -> s (r o)", r=PACK))
 
         q_bf = [tile("q_bf%d" % g, [P, width, PACK], BF16) for g, width in enumerate(q_widths)]
         q_codes = [tile("q_codes%d" % g, [P, width], U32) for g, width in enumerate(q_widths)]
@@ -81,7 +81,8 @@ def tile_rows_kb_cap_kernel(tc, qT, kT, t, v, kb, out):
         y_banks = [ps.tile([P, Y_SLOTS, E], F32, name="y%d" % b) for b in range(Y_BANKS)]
 
         def pieces(u):
-            return [(0, QT // 2), (QT // 2, QT)] if u == LAST else [(0, QT)]
+            count = PIECES[u]
+            return [(i * QT // count, (i + 1) * QT // count) for i in range(count)]
 
         capped = {
             (h, c): tile("capped%d_%d" % (h, c), [P, PACK, (end - first) * QT], F32)
@@ -106,8 +107,10 @@ def tile_rows_kb_cap_kernel(tc, qT, kT, t, v, kb, out):
         def quantise(codes, scales, words):
             nc.vector.quantize_mx(out=codes.bitcast(FP8X4), scales=scales, in_=words.rearrange("p c j -> p (c j)"))
 
-        def prepare_q(g):
+        def pack_q(g):
             nc.vector.tensor_copy(out=side_by_side(q_bf[g][:]), in_=by_rows(q_raw[g][:]))
+
+        def quantise_q(g):
             quantise(q_codes[g][:], q_scales[g][:], q_bf[g][:])
 
         def k_views(g, r0, r1):
@@ -134,11 +137,13 @@ def tile_rows_kb_cap_kernel(tc, qT, kT, t, v, kb, out):
             width = (end - first) * QT
             per_bank = NQ // width
             if c == 0:
-                bank, slot = FIRST_SPAN_BANK[h][r], r
+                bank, slot = r % SCORE_BANKS[h], r
             elif per_bank == 1:
-                bank, slot = (r + 1) % SCORE_BANKS[h], 0
+                bank, slot = r % SCORE_BANKS[h], 0
+            elif c == 2:
+                bank, slot = 0, r
             else:
-                bank, slot = divmod(r, per_bank)
+                slot, bank = divmod(r, SCORE_BANKS[h])
             return score_banks[h][bank][:, slot * width : (slot + 1) * width]
 
         def scores(h, c, r):
@@ -224,7 +229,8 @@ def tile_rows_kb_cap_kernel(tc, qT, kT, t, v, kb, out):
             queue = nc.scalar if u == LAST - 1 else nc.sync
             queue.dma_start(out=out[h, x * QT : (x + 1) * QT, :], in_=result[u][:])
 
-        prepare_q(0)
+        pack_q(0)
+        quantise_q(0)
         pack_k(0, 0, 2)
         pack_k(0, 2, 4)
         pack_k(1, 0, 1)
@@ -239,67 +245,74 @@ def tile_rows_kb_cap_kernel(tc, qT, kT, t, v, kb, out):
                 cap(h, 0, r)
         quantise_k(2)
         quantise_k(3)
-        rest_of_first_span = ((0, 2), (0, 3), (1, 3), (1, 2))
-        for h, r in rest_of_first_span:
-            scores(h, 0, r)
-        for h, r in rest_of_first_span:
-            cap(h, 0, r)
+        for h in range(H):
+            for r in (2, 3):
+                scores(h, 0, r)
+        for h in range(H):
+            for r in (2, 3):
+                cap(h, 0, r)
         exponentiate(0)
         exponentiate(1)
-
-        prepare_q(1)
-        prepare_q(2)
-        for r in range(PACK):
-            scores(1, 1, r)
-        for r in range(SCORE_BANKS[0]):
+        pack_q(1)
+        pack_q(2)
+        quantise_q(1)
+        quantise_q(2)
+        for r in range(3):
             scores(0, 1, r)
-        for r in range(PACK):
-            cap(1, 1, r)
-        for r in range(PACK):
-            scores(1, 2, r)
+        scores(1, 1, 0)
         cap(0, 1, 0)
         scores(0, 1, 3)
-        for h in range(H):
-            weigh(h)
-            pack_v(h)
-        quantise_w(0, 2)
-        quantise(v_codes[:], v_scales[:], v_bf[:])
-        values(0)
-        values(1)
-
-        exponentiate(2)
+        scores(1, 1, 1)
         cap(0, 1, 1)
-        exponentiate(3)
         cap(0, 1, 2)
+        cap(1, 1, 0)
         cap(0, 1, 3)
-        cap(1, 2, 0)
-        for u in (4, 5, 6):
-            exponentiate(u)
-        for r in range(1, PACK):
-            cap(1, 2, r)
-
-        weigh(2)
-        invert(0, 2)
-        quantise_and_multiply(2)
-        weigh(3)
+        cap(1, 1, 1)
+        exponentiate(2)
+        pack_v(0)
+        pack_v(1)
+        weigh(0)
+        quantise(v_codes[:], v_scales[:], v_bf[:])
+        quantise_and_multiply(0)
+        weigh(1)
+        scores(1, 1, 2)
+        quantise_and_multiply(1)
+        scores(1, 1, 3)
+        invert(0)
         divide(0)
+        invert(1)
+        exponentiate(3)
+        cap(1, 1, 2)
+        weigh(2)
+        weigh(3)
+        for r in range(PACK):
+            scores(1, 2, r)
+        quantise_and_multiply(2)
         divide(1)
         quantise_and_multiply(3)
+        cap(1, 1, 3)
+        exponentiate(4)
+        exponentiate(5)
+        exponentiate(6, 0)
+        for r in range(PACK):
+            cap(1, 2, r)
+        exponentiate(6, 1)
+        exponentiate(7, 0)
+        exponentiate(7, 1)
         weigh(4)
-        invert(2, 2)
-        divide(2)
-        exponentiate(LAST, 0)
-        exponentiate(LAST, 1)
-        divide(3)
         weigh(5)
+        invert(2, 2)
         quantise_and_multiply(4)
-        weigh(6)
+        divide(2)
+        divide(3)
+        weigh(6, 0)
         quantise_and_multiply(5)
-        weigh(LAST, 0)
-        weigh(LAST, 1)
+        weigh(6, 1)
+        weigh(7, 0)
+        weigh(7, 1)
         quantise_and_multiply(6)
         invert(4, 2)
-        quantise_and_multiply(LAST)
+        quantise_and_multiply(7)
         divide(4)
         divide(5)
         for u in (LAST - 1, LAST):

@@ -42,9 +42,10 @@ def tile_rows_kb_cap_kernel(tc, qT, kT, t, v, kb, out):
             return sb.tile(shape, dtype, name=name, align_bytes=64)
 
         q_widths = [(end - first) * QT for first, end in Q_LOADS]
-        kb_raw = tile("kb_raw", [P, PACK], F32)
+        kb_rows = tile("kb_rows", [P, P], F32)
+        kb_dealt = tile("kb_dealt", [P, PACK, 32], F32)
         t_sb = tile("t_sb", [P, PACK], F32)
-        kb_over_cap = tile("kb_over_cap", [P, PACK], F32)
+        kb_over_cap = tile("kb_over_cap", [P, PACK, 32], F32)
         q_raw = [tile("q_raw%d" % g, [P, PACK, width], F32) for g, width in enumerate(q_widths)]
         k_raw = [tile("k_raw%d" % g, [P, 2, N], F32) for g in range(2)]
         v_raw = tile("v_raw", [P, H, PACK, E], F32)
@@ -56,10 +57,10 @@ def tile_rows_kb_cap_kernel(tc, qT, kT, t, v, kb, out):
             first, end = Q_LOADS[g]
             nc.sync.dma_start(out=q_raw[g][:], in_=q_rows[:, :, first * QT : end * QT])
 
+        nc.scalar.dma_start(out=kb_rows[0:P:32, :], in_=kb.rearrange("(g n) o -> g (n o)", n=P))
         load_q(0)
         for g in range(2):
             nc.sync.dma_start(out=k_raw[g][:], in_=k_rows[:, 2 * g : 2 * g + 2, :])
-        nc.sync.dma_start(out=kb_raw[:], in_=kb.rearrange("(s r) o -> s (r o)", r=PACK))
         load_q(1)
         load_q(2)
         nc.sync.dma_start(out=v_raw[:], in_=v.rearrange("h (s r) e -> s h r e", r=PACK))
@@ -167,7 +168,7 @@ def tile_rows_kb_cap_kernel(tc, qT, kT, t, v, kb, out):
                 out=capped[h, c][:, r, :],
                 in_=score_place(h, c, r),
                 func=ACT.Tanh,
-                bias=kb_over_cap[:, r : r + 1],
+                bias=kb_over_cap[:, r, 0:1],
                 scale=1.0 / CAP,
             )
 
@@ -229,14 +230,26 @@ def tile_rows_kb_cap_kernel(tc, qT, kT, t, v, kb, out):
             queue = nc.scalar if u == LAST - 1 else nc.sync
             queue.dma_start(out=out[h, x * QT : (x + 1) * QT, :], in_=result[u][:])
 
+        nc.vector.memset(kb_dealt[:], 0.0)
         pack_q(0)
         quantise_q(0)
+        for g in range(P // 32):
+            live = slice(32 * g, 32 * g + 1)
+            nc.vector.tensor_scalar(
+                out=kb_dealt[live, :, :],
+                in0=kb_rows[live, :].rearrange("p (i r) -> p r i", r=PACK),
+                scalar1=1.0 / CAP,
+                scalar2=None,
+                op0=ALU.mult,
+            )
         pack_k(0, 0, 2)
+        nc.vector.transpose(
+            out=kb_over_cap[:].rearrange("p r i -> p (r i)"), in_=kb_dealt[:].rearrange("p r i -> p (r i)")
+        )
         pack_k(0, 2, 4)
         pack_k(1, 0, 1)
         pack_k(1, 1, 2)
         pack_k_on_scalar(1, 2, 4)
-        nc.scalar.mul(kb_over_cap[:], kb_raw[:], 1.0 / CAP)
         for r, heads in ((0, (0, 1)), (1, (1, 0))):
             quantise_k(r)
             for h in heads:

@@ -57,8 +57,8 @@ def tile_rows_kb_cap_kernel(tc, qT, kT, t, v, kb, out):
             first, end = Q_LOADS[g]
             nc.sync.dma_start(out=q_raw[g][:], in_=q_rows[:, :, first * QT : end * QT])
 
-        nc.scalar.dma_start(out=kb_rows[0:P:32, :], in_=kb.rearrange("(g n) o -> g (n o)", n=P))
         load_q(0)
+        nc.sync.dma_start(out=kb_rows[0:P:32, :], in_=kb.rearrange("(g n) o -> g (n o)", n=P))
         for g in range(2):
             nc.sync.dma_start(out=k_raw[g][:], in_=k_rows[:, 2 * g : 2 * g + 2, :])
         load_q(1)
@@ -246,7 +246,7 @@ def tile_rows_kb_cap_kernel(tc, qT, kT, t, v, kb, out):
         nc.vector.transpose(
             out=kb_over_cap[:].rearrange("p r i -> p (r i)"), in_=kb_dealt[:].rearrange("p r i -> p (r i)")
         )
-        pack_k(0, 2, 4)
+        pack_k_on_scalar(0, 2, 4)
         pack_k(1, 0, 1)
         pack_k(1, 1, 2)
         pack_k_on_scalar(1, 2, 4)

@@ -15,20 +15,24 @@ ACT = mybir.ActivationFunctionType
 ALU = mybir.AluOpType
 
 P = 128
+QUADRANT = 32
+BANK = 512
 PACK = 4
 ROWS = D // PACK
 QT = 128
 RUN = 2
+K_SPLIT = 48
 
 Q_LOADS = [(0, 1), (1, 3), (3, 4)]
-SPANS = [[(0, 1), (1, 4)], [(0, 1), (1, 3), (3, 4)]]
-UNITS = [(h, c, x) for h, c in ((0, 0), (1, 0), (0, 1), (1, 1), (1, 2)) for x in range(*SPANS[h][c])]
+SPANS = [(0, 0, 1), (1, 0, 1), (0, 1, 4), (1, 1, 3), (1, 3, 4)]
+OPEN0, OPEN1, WIDE, MIDDLE, CLOSE = range(len(SPANS))
+UNITS = [(c, x) for c, (h, first, end) in enumerate(SPANS) for x in range(first, end)]
 LAST = len(UNITS) - 1
 SCORE_BANKS = [3, 2]
-Y_PLACES = [(0, 0), (1, 0), (0, 1), (0, 2), (2, 0), (2, 1), (0, 3), (1, 1)]
-Y_BANKS, Y_SLOTS = 3, 4
+Y_BANKS = 3
+Y_GROUPS = [(0,), (1,), (2, 3), (4, 5), (6,), (7,)]
+Y_SLOTS = BANK // E
 SCALAR_DIVIDES = range(2, LAST)
-PIECES = [1, 1, 1, 1, 1, 1, 2, 2]
 
 
 def tile_rows_kb_cap_kernel(tc, qT, kT, t, v, kb, out):
@@ -42,10 +46,10 @@ def tile_rows_kb_cap_kernel(tc, qT, kT, t, v, kb, out):
             return sb.tile(shape, dtype, name=name, align_bytes=64)
 
         q_widths = [(end - first) * QT for first, end in Q_LOADS]
-        kb_rows = tile("kb_rows", [P, P], F32)
-        kb_dealt = tile("kb_dealt", [P, PACK, 32], F32)
+        kb_rows = tile("kb_rows", [P, QUADRANT * PACK], F32)
+        kb_dealt = tile("kb_dealt", [P, PACK, QUADRANT], F32)
+        kb_over_cap = tile("kb_over_cap", [P, PACK, QUADRANT], F32)
         t_sb = tile("t_sb", [P, PACK], F32)
-        kb_over_cap = tile("kb_over_cap", [P, PACK, 32], F32)
         q_raw = [tile("q_raw%d" % g, [P, PACK, width], F32) for g, width in enumerate(q_widths)]
         k_raw = [tile("k_raw%d" % g, [P, 2, N], F32) for g in range(2)]
         v_raw = tile("v_raw", [P, H, PACK, E], F32)
@@ -58,7 +62,7 @@ def tile_rows_kb_cap_kernel(tc, qT, kT, t, v, kb, out):
             nc.sync.dma_start(out=q_raw[g][:], in_=q_rows[:, :, first * QT : end * QT])
 
         load_q(0)
-        nc.sync.dma_start(out=kb_rows[0:P:32, :], in_=kb.rearrange("(g n) o -> g (n o)", n=P))
+        nc.sync.dma_start(out=kb_rows[0:P:QUADRANT, :], in_=kb.rearrange("(g n) o -> g (n o)", n=QUADRANT * PACK))
         for g in range(2):
             nc.sync.dma_start(out=k_raw[g][:], in_=k_rows[:, 2 * g : 2 * g + 2, :])
         load_q(1)
@@ -77,19 +81,21 @@ def tile_rows_kb_cap_kernel(tc, qT, kT, t, v, kb, out):
         v_scales = tile("v_scales", [P, H * E], U8)
 
         score_banks = [
-            [ps.tile([P, NQ], F32, name="score%d_%d" % (h, b)) for b in range(SCORE_BANKS[h])] for h in range(H)
+            [ps.tile([P, BANK], F32, name="score%d_%d" % (h, b)) for b in range(SCORE_BANKS[h])] for h in range(H)
         ]
         y_banks = [ps.tile([P, Y_SLOTS, E], F32, name="y%d" % b) for b in range(Y_BANKS)]
+        y_slot = {}
+        for n, group in enumerate(Y_GROUPS):
+            for u in group:
+                bank = n % Y_BANKS
+                y_slot[u] = (bank, len([b for b, slot in y_slot.values() if b == bank]))
 
         def pieces(u):
-            count = PIECES[u]
-            return [(i * QT // count, (i + 1) * QT // count) for i in range(count)]
+            return [(0, QT // 2), (QT // 2, QT)] if u >= LAST - 1 else [(0, QT)]
 
-        capped = {
-            (h, c): tile("capped%d_%d" % (h, c), [P, PACK, (end - first) * QT], F32)
-            for h in range(H)
-            for c, (first, end) in enumerate(SPANS[h])
-        }
+        capped = [
+            tile("capped%d" % c, [P, PACK, (end - first) * QT], F32) for c, (h, first, end) in enumerate(SPANS)
+        ]
         prob = {
             (u, a): tile("prob%d_%d" % (u, a), [P, PACK, b - a], F32) for u in range(len(UNITS)) for a, b in pieces(u)
         }
@@ -108,23 +114,43 @@ def tile_rows_kb_cap_kernel(tc, qT, kT, t, v, kb, out):
         def quantise(codes, scales, words):
             nc.vector.quantize_mx(out=codes.bitcast(FP8X4), scales=scales, in_=words.rearrange("p c j -> p (c j)"))
 
+        def deal_kb():
+            for g in range(P // QUADRANT):
+                live = slice(QUADRANT * g, QUADRANT * g + 1)
+                nc.vector.tensor_scalar(
+                    out=kb_dealt[live, :, :],
+                    in0=kb_rows[live, :].rearrange("p (i r) -> p r i", r=PACK),
+                    scalar1=1.0 / CAP,
+                    scalar2=None,
+                    op0=ALU.mult,
+                )
+
+        def turn_kb():
+            nc.vector.transpose(
+                out=kb_over_cap[:].rearrange("p r i -> p (r i)"), in_=kb_dealt[:].rearrange("p r i -> p (r i)")
+            )
+
         def pack_q(g):
             nc.vector.tensor_copy(out=side_by_side(q_bf[g][:]), in_=by_rows(q_raw[g][:]))
 
         def quantise_q(g):
             quantise(q_codes[g][:], q_scales[g][:], q_bf[g][:])
 
-        def k_views(g, r0, r1):
-            words = k_bf[:, r0:r1, :, 2 * g : 2 * g + 2].rearrange("p r s j -> p s j r")
-            rows = k_raw[g][:].rearrange("p j (s r) -> p s j r", r=PACK)[:, :, :, r0:r1]
+        def k_views(g, operands, cols):
+            words = k_bf[:, operands, cols, 2 * g : 2 * g + 2].rearrange("p r s j -> p s j r")
+            rows = k_raw[g][:].rearrange("p j (s r) -> p s j r", r=PACK)[:, cols, :, operands]
             return words, rows
 
-        def pack_k(g, r0, r1):
-            words, rows = k_views(g, r0, r1)
+        def pack_k(g, first, end):
+            words, rows = k_views(g, slice(first, end), slice(0, P))
             nc.vector.tensor_copy(out=words, in_=rows)
 
-        def pack_k_on_scalar(g, r0, r1):
-            words, rows = k_views(g, r0, r1)
+        def pack_late_k_on_vector(g):
+            words, rows = k_views(g, slice(2, PACK), slice(0, K_SPLIT))
+            nc.vector.tensor_copy(out=words, in_=rows)
+
+        def pack_late_k_on_scalar(g):
+            words, rows = k_views(g, slice(2, PACK), slice(K_SPLIT, P))
             nc.scalar.activation(out=words, in_=rows, func=ACT.Copy)
 
         def quantise_k(r):
@@ -133,28 +159,21 @@ def tile_rows_kb_cap_kernel(tc, qT, kT, t, v, kb, out):
         def pack_v(h):
             nc.vector.tensor_copy(out=side_by_side(v_bf[:, h * E : (h + 1) * E, :]), in_=by_rows(v_raw[:, h, :, :]))
 
-        def score_place(h, c, r):
-            first, end = SPANS[h][c]
+        def score_place(c, r):
+            h, first, end = SPANS[c]
             width = (end - first) * QT
-            per_bank = NQ // width
-            if c == 0:
-                bank, slot = r % SCORE_BANKS[h], r
-            elif per_bank == 1:
-                bank, slot = r % SCORE_BANKS[h], 0
-            elif c == 2:
-                bank, slot = 0, r
-            else:
-                slot, bank = divmod(r, SCORE_BANKS[h])
+            turn, bank = divmod(r, SCORE_BANKS[h])
+            slot = turn % (BANK // width)
             return score_banks[h][bank][:, slot * width : (slot + 1) * width]
 
-        def scores(h, c, r):
+        def scores(c, r):
+            h, first, end = SPANS[c]
             rows = slice(h * ROWS, (h + 1) * ROWS)
-            first, end = SPANS[h][c]
             for x in range(first, end):
                 g = [i for i, (a, b) in enumerate(Q_LOADS) if a <= x < b][0]
                 cols = slice((x - Q_LOADS[g][0]) * QT, (x - Q_LOADS[g][0] + 1) * QT)
                 nc.tensor.matmul_mx(
-                    out=score_place(h, c, r)[:, (x - first) * QT : (x - first + 1) * QT],
+                    out=score_place(c, r)[:, (x - first) * QT : (x - first + 1) * QT],
                     lhsT=k_codes[r][rows, :].bitcast(FP8X4),
                     lhsT_scale=k_scales[r][rows, :],
                     rhs=q_codes[g][rows, cols].bitcast(FP8X4),
@@ -163,22 +182,26 @@ def tile_rows_kb_cap_kernel(tc, qT, kT, t, v, kb, out):
                     stop=True,
                 )
 
-        def cap(h, c, r):
+        def cap(c, r):
             nc.scalar.activation(
-                out=capped[h, c][:, r, :],
-                in_=score_place(h, c, r),
+                out=capped[c][:, r, :],
+                in_=score_place(c, r),
                 func=ACT.Tanh,
                 bias=kb_over_cap[:, r, 0:1],
                 scale=1.0 / CAP,
             )
 
+        def scores_then_cap(steps):
+            for c, r in steps:
+                scores(c, r)
+            for c, r in steps:
+                cap(c, r)
+
         def exponentiate(u, piece=0):
-            h, c, x = UNITS[u]
+            c, x = UNITS[u]
             a, b = pieces(u)[piece]
-            start = (x - SPANS[h][c][0]) * QT
-            nc.scalar.activation(
-                out=prob[u, a][:], in_=capped[h, c][:, :, start + a : start + b], func=ACT.Exp, scale=CAP
-            )
+            start = (x - SPANS[c][1]) * QT
+            nc.scalar.activation(out=prob[u, a][:], in_=capped[c][:, :, start + a : start + b], func=ACT.Exp, scale=CAP)
 
         def weigh(u, piece=0):
             a, b = pieces(u)[piece]
@@ -189,18 +212,15 @@ def tile_rows_kb_cap_kernel(tc, qT, kT, t, v, kb, out):
                 op=ALU.mult,
             )
 
-        def quantise_w(u, count=1):
-            cols = slice(u * QT, (u + count) * QT)
-            quantise(w_codes[:, cols], w_scales[:, cols], w_bf[:, cols, :])
-
         def y_place(u):
-            bank, slot = Y_PLACES[u]
+            bank, slot = y_slot[u]
             return y_banks[bank][:, slot, :]
 
-        def values(u):
-            h = UNITS[u][0]
+        def quantise_and_multiply(u):
+            h = SPANS[UNITS[u][0]][0]
             queries = slice(u * QT, (u + 1) * QT)
             cols = slice(h * E, (h + 1) * E)
+            quantise(w_codes[:, queries], w_scales[:, queries], w_bf[:, queries, :])
             nc.tensor.matmul_mx(
                 out=y_place(u),
                 lhsT=w_codes[:, queries].bitcast(FP8X4),
@@ -211,16 +231,13 @@ def tile_rows_kb_cap_kernel(tc, qT, kT, t, v, kb, out):
                 stop=True,
             )
 
-        def quantise_and_multiply(u):
-            quantise_w(u)
-            values(u)
-
-        def invert(u, count=1):
-            bank, slot = Y_PLACES[u]
+        def invert(u):
+            count = len([group for group in Y_GROUPS if group[0] == u][0])
+            bank, slot = y_slot[u]
             nc.vector.reciprocal(out=inverse[:, u : u + count], in_=y_banks[bank][:, slot : slot + count, E - 1])
 
         def divide(u):
-            h, c, x = UNITS[u]
+            c, x = UNITS[u]
             if u in SCALAR_DIVIDES:
                 nc.scalar.activation(out=result[u][:], in_=y_place(u), func=ACT.Copy, scale=inverse[:, u : u + 1])
             else:
@@ -228,104 +245,94 @@ def tile_rows_kb_cap_kernel(tc, qT, kT, t, v, kb, out):
                     out=result[u][:], in0=y_place(u), scalar1=inverse[:, u : u + 1], scalar2=None, op0=ALU.mult
                 )
             queue = nc.scalar if u == LAST - 1 else nc.sync
-            queue.dma_start(out=out[h, x * QT : (x + 1) * QT, :], in_=result[u][:])
+            queue.dma_start(out=out[SPANS[c][0], x * QT : (x + 1) * QT, :], in_=result[u][:])
 
         nc.vector.memset(kb_dealt[:], 0.0)
         pack_q(0)
         quantise_q(0)
-        for g in range(P // 32):
-            live = slice(32 * g, 32 * g + 1)
-            nc.vector.tensor_scalar(
-                out=kb_dealt[live, :, :],
-                in0=kb_rows[live, :].rearrange("p (i r) -> p r i", r=PACK),
-                scalar1=1.0 / CAP,
-                scalar2=None,
-                op0=ALU.mult,
-            )
+        deal_kb()
         pack_k(0, 0, 2)
-        nc.vector.transpose(
-            out=kb_over_cap[:].rearrange("p r i -> p (r i)"), in_=kb_dealt[:].rearrange("p r i -> p (r i)")
-        )
-        pack_k_on_scalar(0, 2, 4)
+        turn_kb()
+        pack_late_k_on_vector(0)
+        pack_late_k_on_scalar(0)
+
         pack_k(1, 0, 1)
         pack_k(1, 1, 2)
-        pack_k_on_scalar(1, 2, 4)
-        for r, heads in ((0, (0, 1)), (1, (1, 0))):
-            quantise_k(r)
-            for h in heads:
-                scores(h, 0, r)
-            for h in heads:
-                cap(h, 0, r)
+        pack_late_k_on_scalar(1)
+        quantise_k(0)
+        pack_late_k_on_vector(1)
+        scores_then_cap([(OPEN0, 0), (OPEN1, 0)])
+        quantise_k(1)
+        scores_then_cap([(OPEN1, 1), (OPEN0, 1)])
         quantise_k(2)
         quantise_k(3)
-        for h in range(H):
-            for r in (2, 3):
-                scores(h, 0, r)
-        for h in range(H):
-            for r in (2, 3):
-                cap(h, 0, r)
+        scores_then_cap([(c, r) for c in (OPEN0, OPEN1) for r in (2, 3)])
         exponentiate(0)
         exponentiate(1)
+
         pack_q(1)
         pack_q(2)
         quantise_q(1)
         quantise_q(2)
-        for r in range(3):
-            scores(0, 1, r)
-        scores(1, 1, 0)
-        cap(0, 1, 0)
-        scores(0, 1, 3)
-        scores(1, 1, 1)
-        cap(0, 1, 1)
-        cap(0, 1, 2)
-        cap(1, 1, 0)
-        cap(0, 1, 3)
-        cap(1, 1, 1)
+        for r in range(SCORE_BANKS[0]):
+            scores(WIDE, r)
+        scores(MIDDLE, 0)
+        cap(WIDE, 0)
+        scores(WIDE, 3)
+        scores(MIDDLE, 1)
+        cap(WIDE, 1)
+        cap(WIDE, 2)
+        cap(MIDDLE, 0)
+        cap(WIDE, 3)
+        cap(MIDDLE, 1)
         exponentiate(2)
-        pack_v(0)
-        pack_v(1)
+
+        for h in range(H):
+            pack_v(h)
         weigh(0)
         quantise(v_codes[:], v_scales[:], v_bf[:])
         quantise_and_multiply(0)
         weigh(1)
-        scores(1, 1, 2)
+        scores(MIDDLE, 2)
         quantise_and_multiply(1)
-        scores(1, 1, 3)
+        scores(MIDDLE, 3)
         invert(0)
         divide(0)
         invert(1)
+
         exponentiate(3)
-        cap(1, 1, 2)
+        cap(MIDDLE, 2)
+        cap(MIDDLE, 3)
+        for r in range(PACK):
+            scores(CLOSE, r)
         weigh(2)
         weigh(3)
-        for r in range(PACK):
-            scores(1, 2, r)
         quantise_and_multiply(2)
         divide(1)
         quantise_and_multiply(3)
-        cap(1, 1, 3)
         exponentiate(4)
         exponentiate(5)
-        exponentiate(6, 0)
+        exponentiate(LAST - 1, 0)
         for r in range(PACK):
-            cap(1, 2, r)
-        exponentiate(6, 1)
-        exponentiate(7, 0)
-        exponentiate(7, 1)
+            cap(CLOSE, r)
+        exponentiate(LAST - 1, 1)
+        exponentiate(LAST, 0)
+        exponentiate(LAST, 1)
         weigh(4)
         weigh(5)
-        invert(2, 2)
+        invert(2)
         quantise_and_multiply(4)
         divide(2)
         divide(3)
-        weigh(6, 0)
+        weigh(LAST - 1, 0)
         quantise_and_multiply(5)
-        weigh(6, 1)
-        weigh(7, 0)
-        weigh(7, 1)
-        quantise_and_multiply(6)
-        invert(4, 2)
-        quantise_and_multiply(7)
+        weigh(LAST - 1, 1)
+        weigh(LAST, 0)
+        weigh(LAST, 1)
+
+        quantise_and_multiply(LAST - 1)
+        invert(4)
+        quantise_and_multiply(LAST)
         divide(4)
         divide(5)
         for u in (LAST - 1, LAST):

@@ -15,7 +15,6 @@ ACT = mybir.ActivationFunctionType
 ALU = mybir.AluOpType
 
 P = 128
-QUADRANT = 32
 BANK = 512
 PACK = 4
 ROWS = D // PACK
@@ -46,10 +45,9 @@ def tile_rows_kb_cap_kernel(tc, qT, kT, t, v, kb, out):
             return sb.tile(shape, dtype, name=name, align_bytes=64)
 
         q_widths = [(end - first) * QT for first, end in Q_LOADS]
-        kb_rows = tile("kb_rows", [P, QUADRANT * PACK], F32)
-        kb_dealt = tile("kb_dealt", [P, PACK, QUADRANT], F32)
-        kb_over_cap = tile("kb_over_cap", [P, PACK, QUADRANT], F32)
+        kb_raw = tile("kb_raw", [P, PACK], F32)
         t_sb = tile("t_sb", [P, PACK], F32)
+        kb_over_cap = tile("kb_over_cap", [P, PACK], F32)
         q_raw = [tile("q_raw%d" % g, [P, PACK, width], F32) for g, width in enumerate(q_widths)]
         k_raw = [tile("k_raw%d" % g, [P, 2, N], F32) for g in range(2)]
         v_raw = tile("v_raw", [P, H, PACK, E], F32)
@@ -61,8 +59,8 @@ def tile_rows_kb_cap_kernel(tc, qT, kT, t, v, kb, out):
             first, end = Q_LOADS[g]
             nc.sync.dma_start(out=q_raw[g][:], in_=q_rows[:, :, first * QT : end * QT])
 
+        nc.scalar.dma_start(out=kb_raw[:], in_=kb.rearrange("(s r) o -> s (r o)", r=PACK))
         load_q(0)
-        nc.sync.dma_start(out=kb_rows[0:P:QUADRANT, :], in_=kb.rearrange("(g n) o -> g (n o)", n=QUADRANT * PACK))
         for g in range(2):
             nc.sync.dma_start(out=k_raw[g][:], in_=k_rows[:, 2 * g : 2 * g + 2, :])
         load_q(1)
@@ -113,22 +111,6 @@ def tile_rows_kb_cap_kernel(tc, qT, kT, t, v, kb, out):
 
         def quantise(codes, scales, words):
             nc.vector.quantize_mx(out=codes.bitcast(FP8X4), scales=scales, in_=words.rearrange("p c j -> p (c j)"))
-
-        def deal_kb():
-            for g in range(P // QUADRANT):
-                live = slice(QUADRANT * g, QUADRANT * g + 1)
-                nc.vector.tensor_scalar(
-                    out=kb_dealt[live, :, :],
-                    in0=kb_rows[live, :].rearrange("p (i r) -> p r i", r=PACK),
-                    scalar1=1.0 / CAP,
-                    scalar2=None,
-                    op0=ALU.mult,
-                )
-
-        def turn_kb():
-            nc.vector.transpose(
-                out=kb_over_cap[:].rearrange("p r i -> p (r i)"), in_=kb_dealt[:].rearrange("p r i -> p (r i)")
-            )
 
         def pack_q(g):
             nc.vector.tensor_copy(out=side_by_side(q_bf[g][:]), in_=by_rows(q_raw[g][:]))
@@ -187,7 +169,7 @@ def tile_rows_kb_cap_kernel(tc, qT, kT, t, v, kb, out):
                 out=capped[c][:, r, :],
                 in_=score_place(c, r),
                 func=ACT.Tanh,
-                bias=kb_over_cap[:, r, 0:1],
+                bias=kb_over_cap[:, r : r + 1],
                 scale=1.0 / CAP,
             )
 
@@ -247,14 +229,12 @@ def tile_rows_kb_cap_kernel(tc, qT, kT, t, v, kb, out):
             queue = nc.scalar if u == LAST - 1 else nc.sync
             queue.dma_start(out=out[SPANS[c][0], x * QT : (x + 1) * QT, :], in_=result[u][:])
 
-        nc.vector.memset(kb_dealt[:], 0.0)
         pack_q(0)
         quantise_q(0)
-        deal_kb()
         pack_k(0, 0, 2)
-        turn_kb()
         pack_late_k_on_vector(0)
         pack_late_k_on_scalar(0)
+        nc.scalar.mul(kb_over_cap[:], kb_raw[:], 1.0 / CAP)
 
         pack_k(1, 0, 1)
         pack_k(1, 1, 2)

@@ -25,10 +25,11 @@ K_SPLIT = 48
 Q_LOADS = [(0, 1), (1, 3), (3, 4)]
 SPANS = [(0, 0, 1), (1, 0, 1), (0, 1, 4), (1, 1, 3), (1, 3, 4)]
 OPEN0, OPEN1, WIDE, MIDDLE, CLOSE = range(len(SPANS))
-UNITS = [(c, x) for c, (h, first, end) in enumerate(SPANS) for x in range(first, end)]
+UNITS = [(c, x) for c in (OPEN1, OPEN0, WIDE, MIDDLE, CLOSE) for x in range(SPANS[c][1], SPANS[c][2])]
 LAST = len(UNITS) - 1
 SCORE_BANKS = [3, 2]
 Y_BANKS = 3
+OPEN_PLACES = [[(0, 0), (1, 0), (2, 0), (2, 1)], [(0, 0), (0, 1), (1, 0), (1, 1)]]
 Y_GROUPS = [(0,), (1,), (2, 3), (4, 5), (6,), (7,)]
 Y_SLOTS = BANK // E
 SCALAR_DIVIDES = range(2, LAST)
@@ -60,11 +61,10 @@ def tile_rows_kb_cap_kernel(tc, qT, kT, t, v, kb, out):
             nc.sync.dma_start(out=q_raw[g][:], in_=q_rows[:, :, first * QT : end * QT])
 
         nc.scalar.dma_start(out=kb_raw[:], in_=kb.rearrange("(s r) o -> s (r o)", r=PACK))
-        load_q(0)
         for g in range(2):
             nc.sync.dma_start(out=k_raw[g][:], in_=k_rows[:, 2 * g : 2 * g + 2, :])
-        load_q(1)
-        load_q(2)
+        for g in range(len(Q_LOADS)):
+            load_q(g)
         nc.sync.dma_start(out=v_raw[:], in_=v.rearrange("h (s r) e -> s h r e", r=PACK))
         nc.sync.dma_start(out=t_sb[:], in_=t.rearrange("(s r) o -> s (r o)", r=PACK))
 
@@ -144,8 +144,11 @@ def tile_rows_kb_cap_kernel(tc, qT, kT, t, v, kb, out):
         def score_place(c, r):
             h, first, end = SPANS[c]
             width = (end - first) * QT
-            turn, bank = divmod(r, SCORE_BANKS[h])
-            slot = turn % (BANK // width)
+            if c in (OPEN0, OPEN1):
+                bank, slot = OPEN_PLACES[h][r]
+            else:
+                turn, bank = divmod(r, SCORE_BANKS[h])
+                slot = turn % (BANK // width)
             return score_banks[h][bank][:, slot * width : (slot + 1) * width]
 
         def scores(c, r):
@@ -229,24 +232,21 @@ def tile_rows_kb_cap_kernel(tc, qT, kT, t, v, kb, out):
             queue = nc.scalar if u == LAST - 1 else nc.sync
             queue.dma_start(out=out[SPANS[c][0], x * QT : (x + 1) * QT, :], in_=result[u][:])
 
-        pack_q(0)
-        quantise_q(0)
         pack_k(0, 0, 2)
         pack_late_k_on_vector(0)
         pack_late_k_on_scalar(0)
         nc.scalar.mul(kb_over_cap[:], kb_raw[:], 1.0 / CAP)
-
-        pack_k(1, 0, 1)
-        pack_k(1, 1, 2)
+        pack_k(1, 0, 2)
         pack_late_k_on_scalar(1)
-        quantise_k(0)
         pack_late_k_on_vector(1)
-        scores_then_cap([(OPEN0, 0), (OPEN1, 0)])
+        quantise_k(0)
+        pack_q(0)
         quantise_k(1)
-        scores_then_cap([(OPEN1, 1), (OPEN0, 1)])
+        quantise_q(0)
         quantise_k(2)
         quantise_k(3)
-        scores_then_cap([(c, r) for c in (OPEN0, OPEN1) for r in (2, 3)])
+        opening = [(OPEN0, 0), (OPEN1, 0), (OPEN1, 1), (OPEN0, 1), (OPEN1, 2), (OPEN1, 3), (OPEN0, 2), (OPEN0, 3)]
+        scores_then_cap(opening)
         exponentiate(0)
         exponentiate(1)
 

@@ -112,11 +112,11 @@ def tile_rows_kb_cap_kernel(tc, qT, kT, t, v, kb, out):
         def quantise(codes, scales, words):
             nc.vector.quantize_mx(out=codes.bitcast(FP8X4), scales=scales, in_=words.rearrange("p c j -> p (c j)"))
 
-        def pack_q(g):
-            nc.vector.tensor_copy(out=side_by_side(q_bf[g][:]), in_=by_rows(q_raw[g][:]))
+        def pack_q(g, cols=slice(None)):
+            nc.vector.tensor_copy(out=side_by_side(q_bf[g][:, cols, :]), in_=by_rows(q_raw[g][:, :, cols]))
 
-        def quantise_q(g):
-            quantise(q_codes[g][:], q_scales[g][:], q_bf[g][:])
+        def quantise_q(g, cols=slice(None)):
+            quantise(q_codes[g][:, cols], q_scales[g][:, cols], q_bf[g][:, cols, :])
 
         def k_views(g, operands, cols):
             words = k_bf[:, operands, cols, 2 * g : 2 * g + 2].rearrange("p r s j -> p s j r")
@@ -151,10 +151,10 @@ def tile_rows_kb_cap_kernel(tc, qT, kT, t, v, kb, out):
                 slot = turn % (BANK // width)
             return score_banks[h][bank][:, slot * width : (slot + 1) * width]
 
-        def scores(c, r):
+        def scores(c, r, tiles=range(NQ // QT)):
             h, first, end = SPANS[c]
             rows = slice(h * ROWS, (h + 1) * ROWS)
-            for x in range(first, end):
+            for x in [x for x in range(first, end) if x in tiles]:
                 g = [i for i, (a, b) in enumerate(Q_LOADS) if a <= x < b][0]
                 cols = slice((x - Q_LOADS[g][0]) * QT, (x - Q_LOADS[g][0] + 1) * QT)
                 nc.tensor.matmul_mx(
@@ -201,11 +201,18 @@ def tile_rows_kb_cap_kernel(tc, qT, kT, t, v, kb, out):
             bank, slot = y_slot[u]
             return y_banks[bank][:, slot, :]
 
+        def quantise_w(u, a=0, b=QT):
+            queries = slice(u * QT + a, u * QT + b)
+            quantise(w_codes[:, queries], w_scales[:, queries], w_bf[:, queries, :])
+
         def quantise_and_multiply(u):
+            quantise_w(u)
+            multiply(u)
+
+        def multiply(u):
             h = SPANS[UNITS[u][0]][0]
             queries = slice(u * QT, (u + 1) * QT)
             cols = slice(h * E, (h + 1) * E)
-            quantise(w_codes[:, queries], w_scales[:, queries], w_bf[:, queries, :])
             nc.tensor.matmul_mx(
                 out=y_place(u),
                 lhsT=w_codes[:, queries].bitcast(FP8X4),
@@ -236,13 +243,14 @@ def tile_rows_kb_cap_kernel(tc, qT, kT, t, v, kb, out):
         pack_late_k_on_vector(0)
         pack_late_k_on_scalar(0)
         nc.scalar.mul(kb_over_cap[:], kb_raw[:], 1.0 / CAP)
-        pack_k(1, 0, 2)
+        pack_k(1, 0, 1)
+        pack_k(1, 1, 2)
         pack_late_k_on_scalar(1)
-        pack_late_k_on_vector(1)
         quantise_k(0)
         pack_q(0)
-        quantise_k(1)
+        pack_late_k_on_vector(1)
         quantise_q(0)
+        quantise_k(1)
         quantise_k(2)
         quantise_k(3)
         opening = [(OPEN0, 0), (OPEN1, 0), (OPEN1, 1), (OPEN0, 1), (OPEN1, 2), (OPEN1, 3), (OPEN0, 2), (OPEN0, 3)]
@@ -250,12 +258,17 @@ def tile_rows_kb_cap_kernel(tc, qT, kT, t, v, kb, out):
         exponentiate(0)
         exponentiate(1)
 
-        pack_q(1)
+        tiles = [slice(0, QT), slice(QT, 2 * QT)]
+        pack_q(1, tiles[0])
+        pack_q(1, tiles[1])
+        quantise_q(1, tiles[0])
         pack_q(2)
-        quantise_q(1)
+        quantise_q(1, tiles[1])
         quantise_q(2)
-        for r in range(SCORE_BANKS[0]):
-            scores(WIDE, r)
+        for x in range(SPANS[WIDE][1], SPANS[WIDE][2]):
+            scores(WIDE, 0, [x])
+            scores(WIDE, 1, [x])
+        scores(WIDE, 2)
         scores(MIDDLE, 0)
         cap(WIDE, 0)
         scores(WIDE, 3)
@@ -311,8 +324,10 @@ def tile_rows_kb_cap_kernel(tc, qT, kT, t, v, kb, out):
         weigh(LAST, 1)
 
         quantise_and_multiply(LAST - 1)
+        quantise_w(LAST, 0, QT // 2)
+        quantise_w(LAST, QT // 2, QT)
+        multiply(LAST)
         invert(4)
-        quantise_and_multiply(LAST)
         divide(4)
         divide(5)
         for u in (LAST - 1, LAST):

@@ -20,7 +20,7 @@ PACK = 4
 ROWS = D // PACK
 QT = 128
 RUN = 2
-K_SPLIT = 48
+K_SPLIT = [80, 48]
 
 Q_LOADS = [(0, 1), (1, 3), (3, 4)]
 SPANS = [(0, 0, 1), (1, 0, 1), (0, 1, 4), (1, 1, 3), (1, 3, 4)]
@@ -128,11 +128,11 @@ def tile_rows_kb_cap_kernel(tc, qT, kT, t, v, kb, out):
             nc.vector.tensor_copy(out=words, in_=rows)
 
         def pack_late_k_on_vector(g):
-            words, rows = k_views(g, slice(2, PACK), slice(0, K_SPLIT))
+            words, rows = k_views(g, slice(2, PACK), slice(0, K_SPLIT[g]))
             nc.vector.tensor_copy(out=words, in_=rows)
 
         def pack_late_k_on_scalar(g):
-            words, rows = k_views(g, slice(2, PACK), slice(K_SPLIT, P))
+            words, rows = k_views(g, slice(2, PACK), slice(K_SPLIT[g], P))
             nc.scalar.activation(out=words, in_=rows, func=ACT.Copy)
 
         def quantise_k(r):

from contextlib import ExitStack

import concourse.mybir as mybir

H, D, NQ, N, E = 2, 256, 512, 512, 128
CAP = 2.0
FLOPS = 2 * H * N * NQ * D + 2 * H * NQ * N * E

F32 = mybir.dt.float32
BF16 = mybir.dt.bfloat16
U32 = mybir.dt.uint32
U8 = mybir.dt.uint8
FP8X4 = mybir.dt.float8_e4m3fn_x4
ACT = mybir.ActivationFunctionType
ALU = mybir.AluOpType

P = 128
BANK = 512
PACK = 4
ROWS = D // PACK
QT = 128
RUN = 2
K_SPLIT = [80, 48]

Q_LOADS = [(0, 1), (1, 3), (3, 4)]
SPANS = [(0, 0, 1), (1, 0, 1), (0, 1, 4), (1, 1, 3), (1, 3, 4)]
OPEN0, OPEN1, WIDE, MIDDLE, CLOSE = range(len(SPANS))
UNITS = [(c, x) for c in (OPEN1, OPEN0, WIDE, MIDDLE, CLOSE) for x in range(SPANS[c][1], SPANS[c][2])]
LAST = len(UNITS) - 1
SCORE_BANKS = [3, 2]
Y_BANKS = 3
OPEN_PLACES = [[(0, 0), (1, 0), (2, 0), (2, 1)], [(0, 0), (0, 1), (1, 0), (1, 1)]]
Y_GROUPS = [(0,), (1,), (2, 3), (4, 5), (6,), (7,)]
Y_SLOTS = BANK // E
SCALAR_DIVIDES = range(2, LAST)


def tile_rows_kb_cap_kernel(tc, qT, kT, t, v, kb, out):
    nc = tc.nc
    with ExitStack() as ctx:
        sb = ctx.enter_context(tc.tile_pool(name="sb", bufs=1))
        ps = ctx.enter_context(tc.psum_pool(name="ps", bufs=1))
        ctx.enter_context(tc.manual_schedule())

        def tile(name, shape, dtype):
            return sb.tile(shape, dtype, name=name, align_bytes=64)

        q_widths = [(end - first) * QT for first, end in Q_LOADS]
        kb_raw = tile("kb_raw", [P, PACK], F32)
        t_sb = tile("t_sb", [P, PACK], F32)
        kb_over_cap = tile("kb_over_cap", [P, PACK], F32)
        q_raw = [tile("q_raw%d" % g, [P, PACK, width], F32) for g, width in enumerate(q_widths)]
        k_raw = [tile("k_raw%d" % g, [P, 2, N], F32) for g in range(2)]
        v_raw = tile("v_raw", [P, H, PACK, E], F32)

        q_rows = qT.rearrange("h (p j) n -> (h p) j n", j=PACK)
        k_rows = kT.rearrange("h (p j) n -> (h p) j n", j=PACK)

        def load_q(g):
            first, end = Q_LOADS[g]
            nc.sync.dma_start(out=q_raw[g][:], in_=q_rows[:, :, first * QT : end * QT])

        nc.scalar.dma_start(out=kb_raw[:], in_=kb.rearrange("(s r) o -> s (r o)", r=PACK))
        for g in range(2):
            nc.sync.dma_start(out=k_raw[g][:], in_=k_rows[:, 2 * g : 2 * g + 2, :])
        for g in range(len(Q_LOADS)):
            load_q(g)
        nc.sync.dma_start(out=v_raw[:], in_=v.rearrange("h (s r) e -> s h r e", r=PACK))
        nc.sync.dma_start(out=t_sb[:], in_=t.rearrange("(s r) o -> s (r o)", r=PACK))

        q_bf = [tile("q_bf%d" % g, [P, width, PACK], BF16) for g, width in enumerate(q_widths)]
        q_codes = [tile("q_codes%d" % g, [P, width], U32) for g, width in enumerate(q_widths)]
        q_scales = [tile("q_scales%d" % g, [P, width], U8) for g, width in enumerate(q_widths)]
        k_bf = tile("k_bf", [P, PACK, P, PACK], BF16)
        k_codes = [tile("k_codes%d" % r, [P, P], U32) for r in range(PACK)]
        k_scales = [tile("k_scales%d" % r, [P, P], U8) for r in range(PACK)]
        v_bf = tile("v_bf", [P, H * E, PACK], BF16)
        v_codes = tile("v_codes", [P, H * E], U32)
        v_scales = tile("v_scales", [P, H * E], U8)

        score_banks = [
            [ps.tile([P, BANK], F32, name="score%d_%d" % (h, b)) for b in range(SCORE_BANKS[h])] for h in range(H)
        ]
        y_banks = [ps.tile([P, Y_SLOTS, E], F32, name="y%d" % b) for b in range(Y_BANKS)]
        y_slot = {}
        for n, group in enumerate(Y_GROUPS):
            for u in group:
                bank = n % Y_BANKS
                y_slot[u] = (bank, len([b for b, slot in y_slot.values() if b == bank]))

        def pieces(u):
            return [(0, QT // 2), (QT // 2, QT)] if u >= LAST - 1 else [(0, QT)]

        capped = [
            tile("capped%d" % c, [P, PACK, (end - first) * QT], F32) for c, (h, first, end) in enumerate(SPANS)
        ]
        prob = {
            (u, a): tile("prob%d_%d" % (u, a), [P, PACK, b - a], F32) for u in range(len(UNITS)) for a, b in pieces(u)
        }
        w_bf = tile("w_bf", [P, len(UNITS) * QT, PACK], BF16)
        w_codes = tile("w_codes", [P, len(UNITS) * QT], U32)
        w_scales = tile("w_scales", [P, len(UNITS) * QT], U8)
        inverse = tile("inverse", [P, len(UNITS)], F32)
        result = [tile("result%d" % u, [P, E], F32) for u in range(len(UNITS))]

        def side_by_side(words):
            return words.rearrange("p (c i) j -> p c j i", i=RUN)

        def by_rows(rows):
            return rows.rearrange("p j (c i) -> p c j i", i=RUN)

        def quantise(codes, scales, words):
            nc.vector.quantize_mx(out=codes.bitcast(FP8X4), scales=scales, in_=words.rearrange("p c j -> p (c j)"))

        def pack_q(g, cols=slice(None)):
            nc.vector.tensor_copy(out=side_by_side(q_bf[g][:, cols, :]), in_=by_rows(q_raw[g][:, :, cols]))

        def quantise_q(g, cols=slice(None)):
            quantise(q_codes[g][:, cols], q_scales[g][:, cols], q_bf[g][:, cols, :])

        def k_views(g, operands, cols):
            words = k_bf[:, operands, cols, 2 * g : 2 * g + 2].rearrange("p r s j -> p s j r")
            rows = k_raw[g][:].rearrange("p j (s r) -> p s j r", r=PACK)[:, cols, :, operands]
            return words, rows

        def pack_k(g, first, end):
            words, rows = k_views(g, slice(first, end), slice(0, P))
            nc.vector.tensor_copy(out=words, in_=rows)

        def pack_late_k_on_vector(g):
            words, rows = k_views(g, slice(2, PACK), slice(0, K_SPLIT[g]))
            nc.vector.tensor_copy(out=words, in_=rows)

        def pack_late_k_on_scalar(g):
            words, rows = k_views(g, slice(2, PACK), slice(K_SPLIT[g], P))
            nc.scalar.activation(out=words, in_=rows, func=ACT.Copy)

        def quantise_k(r):
            quantise(k_codes[r][:], k_scales[r][:], k_bf[:, r, :, :])

        def pack_v(h):
            nc.vector.tensor_copy(out=side_by_side(v_bf[:, h * E : (h + 1) * E, :]), in_=by_rows(v_raw[:, h, :, :]))

        def score_place(c, r):
            h, first, end = SPANS[c]
            width = (end - first) * QT
            if c in (OPEN0, OPEN1):
                bank, slot = OPEN_PLACES[h][r]
            else:
                turn, bank = divmod(r, SCORE_BANKS[h])
                slot = turn % (BANK // width)
            return score_banks[h][bank][:, slot * width : (slot + 1) * width]

        def scores(c, r, tiles=range(NQ // QT)):
            h, first, end = SPANS[c]
            rows = slice(h * ROWS, (h + 1) * ROWS)
            for x in [x for x in range(first, end) if x in tiles]:
                g = [i for i, (a, b) in enumerate(Q_LOADS) if a <= x < b][0]
                cols = slice((x - Q_LOADS[g][0]) * QT, (x - Q_LOADS[g][0] + 1) * QT)
                nc.tensor.matmul_mx(
                    out=score_place(c, r)[:, (x - first) * QT : (x - first + 1) * QT],
                    lhsT=k_codes[r][rows, :].bitcast(FP8X4),
                    lhsT_scale=k_scales[r][rows, :],
                    rhs=q_codes[g][rows, cols].bitcast(FP8X4),
                    rhs_scale=q_scales[g][rows, cols],
                    start=True,
                    stop=True,
                )

        def cap(c, r):
            nc.scalar.activation(
                out=capped[c][:, r, :],
                in_=score_place(c, r),
                func=ACT.Tanh,
                bias=kb_over_cap[:, r : r + 1],
                scale=1.0 / CAP,
            )

        def scores_then_cap(steps):
            for c, r in steps:
                scores(c, r)
            for c, r in steps:
                cap(c, r)

        def exponentiate(u, piece=0):
            c, x = UNITS[u]
            a, b = pieces(u)[piece]
            start = (x - SPANS[c][1]) * QT
            nc.scalar.activation(out=prob[u, a][:], in_=capped[c][:, :, start + a : start + b], func=ACT.Exp, scale=CAP)

        def weigh(u, piece=0):
            a, b = pieces(u)[piece]
            nc.vector.tensor_tensor(
                out=side_by_side(w_bf[:, u * QT + a : u * QT + b, :]),
                in0=by_rows(prob[u, a][:]),
                in1=t_sb[:].unsqueeze(1).unsqueeze(3).to_broadcast([P, (b - a) // RUN, PACK, RUN]),
                op=ALU.mult,
            )

        def y_place(u):
            bank, slot = y_slot[u]
            return y_banks[bank][:, slot, :]

        def quantise_w(u, a=0, b=QT):
            queries = slice(u * QT + a, u * QT + b)
            quantise(w_codes[:, queries], w_scales[:, queries], w_bf[:, queries, :])

        def quantise_and_multiply(u):
            quantise_w(u)
            multiply(u)

        def multiply(u):
            h = SPANS[UNITS[u][0]][0]
            queries = slice(u * QT, (u + 1) * QT)
            cols = slice(h * E, (h + 1) * E)
            nc.tensor.matmul_mx(
                out=y_place(u),
                lhsT=w_codes[:, queries].bitcast(FP8X4),
                lhsT_scale=w_scales[:, queries],
                rhs=v_codes[:, cols].bitcast(FP8X4),
                rhs_scale=v_scales[:, cols],
                start=True,
                stop=True,
            )

        def invert(u):
            count = len([group for group in Y_GROUPS if group[0] == u][0])
            bank, slot = y_slot[u]
            nc.vector.reciprocal(out=inverse[:, u : u + count], in_=y_banks[bank][:, slot : slot + count, E - 1])

        def divide(u):
            c, x = UNITS[u]
            if u in SCALAR_DIVIDES:
                nc.scalar.activation(out=result[u][:], in_=y_place(u), func=ACT.Copy, scale=inverse[:, u : u + 1])
            else:
                nc.vector.tensor_scalar(
                    out=result[u][:], in0=y_place(u), scalar1=inverse[:, u : u + 1], scalar2=None, op0=ALU.mult
                )
            queue = nc.scalar if u == LAST - 1 else nc.sync
            queue.dma_start(out=out[SPANS[c][0], x * QT : (x + 1) * QT, :], in_=result[u][:])

        pack_k(0, 0, 2)
        pack_late_k_on_vector(0)
        pack_late_k_on_scalar(0)
        nc.scalar.mul(kb_over_cap[:], kb_raw[:], 1.0 / CAP)
        pack_k(1, 0, 1)
        pack_k(1, 1, 2)
        pack_late_k_on_scalar(1)
        quantise_k(0)
        pack_q(0)
        pack_late_k_on_vector(1)
        quantise_q(0)
        quantise_k(1)
        quantise_k(2)
        quantise_k(3)
        opening = [(OPEN0, 0), (OPEN1, 0), (OPEN1, 1), (OPEN0, 1), (OPEN1, 2), (OPEN1, 3), (OPEN0, 2), (OPEN0, 3)]
        scores_then_cap(opening)
        exponentiate(0)
        exponentiate(1)

        tiles = [slice(0, QT), slice(QT, 2 * QT)]
        pack_q(1, tiles[0])
        pack_q(1, tiles[1])
        quantise_q(1, tiles[0])
        pack_q(2)
        quantise_q(1, tiles[1])
        quantise_q(2)
        for x in range(SPANS[WIDE][1], SPANS[WIDE][2]):
            scores(WIDE, 0, [x])
            scores(WIDE, 1, [x])
        scores(WIDE, 2)
        scores(MIDDLE, 0)
        cap(WIDE, 0)
        scores(WIDE, 3)
        scores(MIDDLE, 1)
        cap(WIDE, 1)
        cap(WIDE, 2)
        cap(MIDDLE, 0)
        cap(WIDE, 3)
        cap(MIDDLE, 1)
        exponentiate(2)

        for h in range(H):
            pack_v(h)
        weigh(0)
        quantise(v_codes[:], v_scales[:], v_bf[:])
        quantise_and_multiply(0)
        weigh(1)
        scores(MIDDLE, 2)
        quantise_and_multiply(1)
        scores(MIDDLE, 3)
        invert(0)
        divide(0)
        invert(1)

        exponentiate(3)
        cap(MIDDLE, 2)
        cap(MIDDLE, 3)
        for r in range(PACK):
            scores(CLOSE, r)
        weigh(2)
        weigh(3)
        quantise_and_multiply(2)
        divide(1)
        quantise_and_multiply(3)
        exponentiate(4)
        exponentiate(5)
        exponentiate(LAST - 1, 0)
        for r in range(PACK):
            cap(CLOSE, r)
        exponentiate(LAST - 1, 1)
        exponentiate(LAST, 0)
        exponentiate(LAST, 1)
        weigh(4)
        weigh(5)
        invert(2)
        quantise_and_multiply(4)
        divide(2)
        divide(3)
        weigh(LAST - 1, 0)
        quantise_and_multiply(5)
        weigh(LAST - 1, 1)
        weigh(LAST, 0)
        weigh(LAST, 1)

        quantise_and_multiply(LAST - 1)
        quantise_w(LAST, 0, QT // 2)
        quantise_w(LAST, QT // 2, QT)
        multiply(LAST)
        invert(4)
        divide(4)
        divide(5)
        for u in (LAST - 1, LAST):
            invert(u)
            divide(u)
